import numpy as np
import ml_dtypes


def mxq(x, axis, fmt="e4m3"):
    dtype, down = {"e4m3": (ml_dtypes.float8_e4m3fn, 7), "e5m2": (ml_dtypes.float8_e5m2, 14)}[fmt]
    v = np.moveaxis(np.asarray(x, np.float32).astype(ml_dtypes.bfloat16).astype(np.float64), axis, -1)
    blocks = v.reshape(v.shape[:-1] + (-1, 32))
    amax = np.abs(blocks).max(-1, keepdims=True)
    byte = np.maximum(np.where(amax > 0, np.frexp(amax)[1] - 1 + 127, 0) - down, 1)
    scale = np.exp2(byte - 127.0)
    codes = (blocks / scale).astype(np.float32).astype(dtype).astype(np.float64)
    return np.moveaxis((codes * scale).reshape(v.shape), -1, axis)


WIDE = False


def mx_kscale(k):
    if not WIDE:
        return np.ones(k)
    levels = np.array([30, -30])
    if k % 512:
        return np.exp2(np.random.permutation(np.resize(levels, k // 32))).repeat(32)
    a = np.empty((k // 512, 16))
    for p in range(k // 512):
        a[p, :8] = np.random.permutation(np.resize(levels, 8))
        for g in range(8):
            far = levels[np.abs(levels - a[p, g]) >= 10]
            a[p, g + 8] = far[np.random.randint(len(far))]
    return np.exp2(a.ravel()).repeat(32)


def f64(x):
    return np.asarray(x).astype(np.float64)


def striped(idx):
    return np.tile(idx.reshape(-1, 16).T, (8, 1)).astype(np.uint16)


def unstriped(offs):
    return offs[:16].T.reshape(-1).astype(np.int64)


def bf(x):
    return np.asarray(x, np.float32).astype(ml_dtypes.bfloat16)


E2M1 = np.array([0.0, 0.5, 1.0, 1.5, 2.0, 3.0, 4.0, 6.0, -0.0, -0.5, -1.0, -1.5, -2.0, -3.0, -4.0, -6.0])


def pack_weight(w, fmt):
    k, n = w.shape
    w = f64(bf(w)).reshape(k // 32, 32, n)
    amax = np.abs(w).max(1)
    if fmt in ("e4m3", "e5m2"):
        byte = np.frexp(amax)[1] - 1 + 127 - (7 if fmt == "e4m3" else 14)
    else:
        mant, ex = np.frexp(amax / 6.0)
        byte = np.where(mant > 0.5, ex, ex - 1) + 127
    byte = np.clip(np.where(amax > 0, byte, 1), 1, 254)
    scaled = (w * np.exp2(127.0 - byte)[:, None, :]).reshape(k, n).astype(np.float32)
    by_word = np.ascontiguousarray(scaled.reshape(k // 512, 128, 4, n).transpose(0, 1, 3, 2))
    if fmt in ("e4m3", "e5m2"):
        words = by_word.astype(ml_dtypes.float8_e4m3fn if fmt == "e4m3" else ml_dtypes.float8_e5m2).view(np.uint8)
    else:
        c = by_word.astype(ml_dtypes.float4_e2m1fn).view(np.uint8) & 0xF
        words = c[..., 0::2] | (c[..., 1::2] << 4)
    return np.ascontiguousarray(words), np.ascontiguousarray(byte.astype(np.uint8).reshape(k // 512, 16, n))


def unpack_weight(words, scales, fmt):
    g, p, n, _ = words.shape
    if fmt in ("e4m3", "e5m2"):
        vals = np.ascontiguousarray(words).view(ml_dtypes.float8_e4m3fn if fmt == "e4m3" else ml_dtypes.float8_e5m2).astype(np.float64)
    else:
        nib = np.empty((g, p, n, 4), np.uint8)
        nib[..., 0::2] = words & 0xF
        nib[..., 1::2] = words >> 4
        vals = E2M1[nib]
    vals = vals * np.repeat(np.exp2(scales.astype(np.float64) - 127.0), 8, axis=1)[..., None]
    return vals.transpose(0, 1, 3, 2).reshape(g * 512, n)


K, T, S, H, N = 2048, 2048, 1024, 1024, 512

def setup_inputs():
    n = np.random.standard_normal
    s = mx_kscale(K)[:, None]
    u = mx_kscale(H)[:, None]
    resid = n((K, T)) * np.exp(0.5 * n((K, T)) + 0.4 * n((1, T)))
    tab_words, tab_scales = pack_weight(resid * s, "e5m2")
    w2_words, w2_scales = pack_weight(n((H, N)) / np.sqrt(H) / u, "e4m3")
    return {
        "tab_words": tab_words,
        "tab_scales": tab_scales,
        "offs": striped(np.random.permutation(T)[:S]),
        "w1": (0.8 * n((K, H)) / np.sqrt(K) / s).astype(np.float32),
        "gain": (np.exp(0.3 * n(H)) * u[:, 0]).astype(np.float32),
        "w2_words": w2_words,
        "w2_scales": w2_scales,
        "b2": (0.5 * n(N)).astype(np.float32),
    }

def reference(tab_words, tab_scales, offs, w1, gain, w2_words, w2_scales, b2):
    v = unpack_weight(tab_words, tab_scales, "e5m2")[:, unstriped(offs)]
    w1q = mxq(f64(w1), 0, "e4m3")
    a = w1q.T @ v
    h = f64(gain)[:, None] * np.square(np.maximum(a, 0.0))
    hq = mxq(h, 0, "e4m3")
    w2 = unpack_weight(w2_words, w2_scales, "e4m3")
    return (w2.T @ hq) + f64(b2)[:, None]

@@ -1,0 +1,225 @@
+from contextlib import ExitStack
+
+import concourse.mybir as mybir
+
+K, T, S, H, N = 2048, 2048, 1024, 1024, 512
+FLOPS = 2 * K * H * S + 2 * H * N * S
+
+F32 = mybir.dt.float32
+BF16 = mybir.dt.bfloat16
+I32 = mybir.dt.int32
+U32 = mybir.dt.uint32
+U16 = mybir.dt.uint16
+U8 = mybir.dt.uint8
+E4M3X4 = mybir.dt.float8_e4m3fn_x4
+E5M2X4 = mybir.dt.float8_e5m2_x4
+ACT = mybir.ActivationFunctionType
+ALU = mybir.AluOpType
+
+P = 128
+PACK = 4
+PASS = P * PACK
+K_PASSES = K // PASS
+R_PASSES = H // PASS
+J_HALVES = S // PASS
+N_TILES = N // P
+
+
+def tile_list_perturbation_program_scores_kernel(
+    tc, tab_words, tab_scales, offs, w1, gain, w2_words, w2_scales, b2, out
+):
+    nc = tc.nc
+    with ExitStack() as ctx:
+        keep = ctx.enter_context(tc.tile_pool(name="keep", bufs=1))
+        ring = ctx.enter_context(tc.tile_pool(name="ring", bufs=2))
+        psum = ctx.enter_context(tc.psum_pool(name="psum", bufs=1))
+
+        offsets = keep.tile([P, S // 16], U16, name="offsets")
+        nc.sync.dma_start(offsets[:], offs)
+
+        tab_sc = keep.tile([P, T], U8, name="tab_sc", align_bytes=64)
+        nc.gpsimd.memset(tab_sc[:].bitcast(I32), 0)
+        for q in range(4):
+            nc.sync.dma_start(
+                out=tab_sc[32 * q : 32 * q + 16, :].bitcast(I32),
+                in_=tab_scales[:, 4 * q : 4 * q + 4, :].bitcast(I32),
+            )
+        gain_sb = keep.tile([P, R_PASSES, PACK], F32, name="gain_sb")
+
+        v_sc = [keep.tile([P, S], U8, name="v_sc%d" % a, align_bytes=64) for a in range(K_PASSES)]
+        for a in range(1, K_PASSES):
+            nc.vector.memset(v_sc[a][:].bitcast(I32), 0)
+        w2_sc = keep.tile([P, N], U8, name="w2_sc", align_bytes=64)
+        nc.vector.memset(w2_sc[:].bitcast(I32), 0)
+
+        nc.vector.tensor_copy(v_sc[0][:], tab_sc[:].indirect(offsets[:]))
+
+        raw = {}
+        tabw = {}
+        w1_q = {}
+        w1_sc = {}
+        v_w = {}
+        grouped = {}
+
+        def load_w1(a, b):
+            raw[a, b] = keep.tile([P, PACK, PASS], F32, name="raw%d" % ((a + 4 * b) % 5))
+            src = w1[PASS * a : PASS * (a + 1), PASS * b : PASS * (b + 1)]
+            nc.sync.dma_start(out=raw[a, b][:], in_=src.rearrange("(p j) c -> p j c", j=PACK))
+
+        def load_tab(a):
+            tabw[a] = ring.tile([P, T], U32, name="tabw", align_bytes=64)
+            nc.sync.dma_start(out=tabw[a][:].bitcast(I32), in_=tab_words[a].rearrange("p t i -> p (t i)").bitcast(I32))
+
+        def cast_w1(a, b, m_split):
+            g = ring.tile([P, PACK, P, PACK], BF16, name="grouped", align_bytes=64, bufs=3)
+            grouped[a, b] = g
+            dst = g[:].rearrange("p t m j -> p m j t")
+            src = raw[a, b][:].rearrange("p j (m t) -> p m j t", t=PACK)
+            if m_split > 0:
+                nc.scalar.activation(out=dst[:, 0:m_split], in_=src[:, 0:m_split], func=ACT.Copy)
+            if m_split < P:
+                nc.vector.tensor_copy(out=dst[:, m_split:P], in_=src[:, m_split:P])
+
+        def quant_w1(a, b):
+            w1_q[a, b] = keep.tile([P, PASS], U32, name="w1q%d%d" % (a, b), align_bytes=64)
+            w1_sc[a, b] = keep.tile([P, PASS], U8, name="w1s%d%d" % (a, b), align_bytes=64)
+            nc.vector.quantize_mx(
+                out=w1_q[a, b][:].bitcast(E4M3X4),
+                scales=w1_sc[a, b][:],
+                in_=grouped[a, b][:].rearrange("p t m j -> p (t m j)"),
+            )
+
+        def gather(a, jh):
+            v_w[a, jh] = keep.tile([P, PASS], U32, name="vw%d%d" % (a, jh), align_bytes=64)
+            nc.vector.tensor_copy(
+                v_w[a, jh][:], tabw[a][:].indirect(offsets[:, 32 * jh : 32 * (jh + 1)])
+            )
+
+        acc = {}
+
+        def stage1(a, b, jh):
+            for t in range(PACK):
+                if a == 0:
+                    acc[b, jh, t] = psum.tile([P, PASS], F32, name="bank%d" % (4 * jh + t))
+                cols = slice(P * t, P * (t + 1))
+                nc.tensor.matmul_mx(
+                    out=acc[b, jh, t][:],
+                    lhsT=w1_q[a, b][:, cols].bitcast(E4M3X4),
+                    lhsT_scale=w1_sc[a, b][:, cols],
+                    rhs=v_w[a, jh][:].bitcast(E5M2X4),
+                    rhs_scale=v_sc[a][:, PASS * jh : PASS * (jh + 1)],
+                    start=(a == 0),
+                    stop=(a == K_PASSES - 1),
+                )
+
+        h_planes = {}
+        h_q = {}
+        h_sc = {}
+
+        def activate(b, jh):
+            hp = ring.tile([P, PACK, PASS], BF16, name="h_planes", align_bytes=64)
+            h_planes[b, jh] = hp
+            for t in range(PACK):
+                r = ring.tile([P, PASS], F32, name="relu", bufs=4)
+                nc.scalar.activation(out=r[:], in_=acc[b, jh, t][:], func=ACT.Relu)
+                nc.vector.scalar_tensor_tensor(
+                    out=hp[:, t, :], in0=r[:], scalar=gain_sb[:, b, t : t + 1], in1=r[:],
+                    op0=ALU.mult, op1=ALU.mult,
+                )
+
+        h_woven = {}
+
+        def weave(b, jh):
+            hw = ring.tile([P, PASS, PACK], BF16, name="h_woven", align_bytes=64)
+            h_woven[b, jh] = hw
+            nc.vector.tensor_copy(
+                out=hw[:].rearrange("p (c i) t -> p c t i", i=4),
+                in_=h_planes[b, jh][:].rearrange("p t (c i) -> p c t i", i=4),
+            )
+
+        def quant_h(b, jh):
+            h_q[b, jh] = keep.tile([P, PASS], U32, name="hq%d%d" % (b, jh), align_bytes=64)
+            h_sc[b, jh] = keep.tile([P, PASS], U8, name="hs%d%d" % (b, jh), align_bytes=64)
+            nc.vector.quantize_mx(
+                out=h_q[b, jh][:].bitcast(E4M3X4),
+                scales=h_sc[b, jh][:],
+                in_=h_woven[b, jh][:].rearrange("p c t -> p (c t)"),
+            )
+
+        for a in range(K_PASSES):
+            load_w1(a, 0)
+            if a == 2:
+                for a2 in range(1, K_PASSES):
+                    nc.sync.dma_start(
+                        out=v_sc[a2][0:100, :].bitcast(I32), in_=v_sc[0][4 * a2 : 4 * a2 + 100, :].bitcast(I32)
+                    )
+            load_tab(a)
+            cast_w1(a, 0, P)
+            quant_w1(a, 0)
+            for jh in range(J_HALVES):
+                gather(a, jh)
+        for a in range(K_PASSES):
+            for jh in range(J_HALVES):
+                stage1(a, 0, jh)
+        nc.sync.dma_start(out=gain_sb[:], in_=gain.rearrange("(b p t) -> p b t", b=R_PASSES, t=PACK))
+        for a in range(K_PASSES):
+            load_w1(a, 1)
+        w2_w = keep.tile([P, R_PASSES, N], U32, name="w2_w", align_bytes=64)
+        nc.sync.dma_start(out=w2_w[:].bitcast(I32), in_=w2_words.rearrange("a p c i -> p a (c i)").bitcast(I32))
+        for q in range(4):
+            nc.sync.dma_start(
+                out=w2_sc[32 * q : 32 * q + 8, :].bitcast(I32),
+                in_=w2_scales[:, 4 * q : 4 * q + 4, :].bitcast(I32),
+            )
+        b2_sb = keep.tile([P, N_TILES], F32, name="b2_sb")
+        with nc.allow_non_contiguous_dma(reason="one bias value a partition"):
+            nc.sync.dma_start(out=b2_sb[:], in_=b2.rearrange("(c p) -> p c", p=P))
+
+        def stage2(jh):
+            for c in range(N_TILES):
+                o = psum.tile([P, PASS], F32, name="bank%d" % (4 * jh + c))
+                cols = slice(P * c, P * (c + 1))
+                for b in range(R_PASSES):
+                    nc.tensor.matmul_mx(
+                        out=o[:],
+                        lhsT=w2_w[:, b, cols].bitcast(E4M3X4),
+                        lhsT_scale=w2_sc[4 * b : P, cols],
+                        rhs=h_q[b, jh][:].bitcast(E4M3X4),
+                        rhs_scale=h_sc[b, jh][:],
+                        start=(b == 0),
+                        stop=(b == R_PASSES - 1),
+                    )
+                res = ring.tile([P, PASS], F32, name="res", bufs=8)
+                if jh == 0 or c % 2 == 0:
+                    nc.scalar.activation(out=res[:], in_=o[:], func=ACT.Identity, bias=b2_sb[:, c : c + 1])
+                else:
+                    nc.vector.tensor_scalar(
+                        out=res[:], in0=o[:], scalar1=b2_sb[:, c : c + 1], scalar2=None, op0=ALU.add
+                    )
+                nc.sync.dma_start(out=out[cols, PASS * jh : PASS * (jh + 1)], in_=res[:])
+
+        activate(0, 0)
+        cast_w1(0, 1, P)
+        weave(0, 0)
+        quant_w1(0, 1)
+        activate(0, 1)
+        quant_h(0, 0)
+        cast_w1(1, 1, P)
+        weave(0, 1)
+        quant_w1(1, 1)
+        cast_w1(2, 1, P)
+        quant_h(0, 1)
+        quant_w1(2, 1)
+        cast_w1(3, 1, 48)
+        quant_w1(3, 1)
+        for a in range(K_PASSES):
+            for jh in range(J_HALVES):
+                stage1(a, 1, jh)
+        activate(1, 0)
+        weave(1, 0)
+        activate(1, 1)
+        quant_h(1, 0)
+        weave(1, 1)
+        stage2(0)
+        quant_h(1, 1)
+        stage2(1)

@@ -23,6 +23,7 @@ K_PASSES = K // PASS
 R_PASSES = H // PASS
 J_HALVES = S // PASS
 N_TILES = N // P
+SIGN_COLS = 64
 
 
 def tile_list_perturbation_program_scores_kernel(
@@ -44,13 +45,43 @@ def tile_list_perturbation_program_scores_kernel(
                 out=tab_sc[32 * q : 32 * q + 16, :].bitcast(I32),
                 in_=tab_scales[:, 4 * q : 4 * q + 4, :].bitcast(I32),
             )
-        gain_sb = keep.tile([P, R_PASSES, PACK], F32, name="gain_sb")
+        gain_sb = keep.tile([P, R_PASSES * PACK], F32, name="gain_sb")
+        nc.sync.dma_start(
+            out=gain_sb[:].rearrange("p (b t) -> p b t", t=PACK),
+            in_=gain.rearrange("(b p t) -> p b t", b=R_PASSES, t=PACK),
+        )
+        G = R_PASSES * PACK
+        g_neg = keep.tile([P, G], F32, name="g_neg")
+        g_abs = keep.tile([P, G], F32, name="g_abs")
+        root0 = keep.tile([P, G], F32, name="root0")
+        guard = keep.tile([P, G], F32, name="guard")
+        recip = keep.tile([P, G], F32, name="recip")
+        quot = keep.tile([P, G], F32, name="quot")
+        twice = keep.tile([P, G], F32, name="twice")
+        root = keep.tile([P, G], F32, name="root")
+        nonneg = keep.tile([P, G], F32, name="nonneg")
+        sign = keep.tile([P, R_PASSES, SIGN_COLS, PACK], BF16, name="sign", align_bytes=64)
+        nc.vector.tensor_scalar(out=g_neg[:], in0=gain_sb[:], scalar1=-1.0, scalar2=None, op0=ALU.mult)
+        nc.vector.tensor_scalar(
+            out=nonneg[:], in0=gain_sb[:], scalar1=0.0, scalar2=2.0, op0=ALU.is_ge, op1=ALU.mult
+        )
+        nc.vector.tensor_tensor(out=g_abs[:], in0=gain_sb[:], in1=g_neg[:], op=ALU.max)
+        nc.scalar.activation(out=root0[:], in_=g_abs[:], func=ACT.Sqrt)
+        for b in range(R_PASSES):
+            nc.vector.tensor_scalar(
+                out=sign[:, b],
+                in0=nonneg[:, PACK * b : PACK * (b + 1)].unsqueeze(1).to_broadcast([P, SIGN_COLS, PACK]),
+                scalar1=-1.0, scalar2=None, op0=ALU.add,
+            )
+        nc.vector.tensor_scalar(out=guard[:], in0=root0[:], scalar1=1e-30, scalar2=None, op0=ALU.max)
+        nc.vector.reciprocal(out=recip[:], in_=guard[:])
+        nc.vector.tensor_tensor(out=quot[:], in0=g_abs[:], in1=recip[:], op=ALU.mult)
+        nc.vector.tensor_tensor(out=twice[:], in0=quot[:], in1=root0[:], op=ALU.add)
+        nc.vector.tensor_scalar(out=root[:], in0=twice[:], scalar1=0.5, scalar2=None, op0=ALU.mult)
 
         v_sc = [keep.tile([P, S], U8, name="v_sc%d" % a, align_bytes=64) for a in range(K_PASSES)]
         for a in range(1, K_PASSES):
             nc.vector.memset(v_sc[a][:].bitcast(I32), 0)
-        w2_sc = keep.tile([P, N], U8, name="w2_sc", align_bytes=64)
-        nc.vector.memset(w2_sc[:].bitcast(I32), 0)
 
         nc.vector.tensor_copy(v_sc[0][:], tab_sc[:].indirect(offsets[:]))
 
@@ -61,33 +92,48 @@ def tile_list_perturbation_program_scores_kernel(
         v_w = {}
         grouped = {}
 
+        def stream_tile(shape, dtype):
+            return ring.tile(shape, dtype, name="stream", align_bytes=64, bufs=5)
+
         def load_w1(a, b):
-            raw[a, b] = keep.tile([P, PACK, PASS], F32, name="raw%d" % ((a + 4 * b) % 5))
-            src = w1[PASS * a : PASS * (a + 1), PASS * b : PASS * (b + 1)]
-            nc.sync.dma_start(out=raw[a, b][:], in_=src.rearrange("(p j) c -> p j c", j=PACK))
+            pieces = 2 if a == K_PASSES - 1 else 1
+            width = PASS // pieces
+            chunk = stream_tile([P, pieces, PACK, width], F32)
+            for u in range(pieces):
+                raw[a, b, u] = chunk[:, u]
+                c0 = PASS * b + width * u
+                src = w1[PASS * a : PASS * (a + 1), c0 : c0 + width]
+                nc.sync.dma_start(out=raw[a, b, u], in_=src.rearrange("(p j) c -> p j c", j=PACK))
 
         def load_tab(a):
-            tabw[a] = ring.tile([P, T], U32, name="tabw", align_bytes=64)
+            tabw[a] = stream_tile([P, T], U32)
             nc.sync.dma_start(out=tabw[a][:].bitcast(I32), in_=tab_words[a].rearrange("p t i -> p (t i)").bitcast(I32))
 
-        def cast_w1(a, b, m_split):
-            g = ring.tile([P, PACK, P, PACK], BF16, name="grouped", align_bytes=64, bufs=3)
+        def cast_w1(a, b, on_scalar):
+            g = ring.tile([P, PACK, P, PACK], BF16, name="to_quantise", align_bytes=64)
             grouped[a, b] = g
-            dst = g[:].rearrange("p t m j -> p m j t")
-            src = raw[a, b][:].rearrange("p j (m t) -> p m j t", t=PACK)
-            if m_split > 0:
-                nc.scalar.activation(out=dst[:, 0:m_split], in_=src[:, 0:m_split], func=ACT.Copy)
-            if m_split < P:
-                nc.vector.tensor_copy(out=dst[:, m_split:P], in_=src[:, m_split:P])
+            groups = P // len(on_scalar)
+            for u, split in enumerate(on_scalar):
+                dst = g[:].rearrange("p t m j -> p m t j")[:, groups * u : groups * (u + 1)]
+                src = raw[a, b, u].rearrange("p j (m t) -> p m t j", t=PACK)
+                if split > 0:
+                    nc.scalar.activation(out=dst[:, 0:split], in_=src[:, 0:split], func=ACT.Copy)
+                if split < groups:
+                    nc.vector.tensor_copy(out=dst[:, split:groups], in_=src[:, split:groups])
 
         def quant_w1(a, b):
             w1_q[a, b] = keep.tile([P, PASS], U32, name="w1q%d%d" % (a, b), align_bytes=64)
             w1_sc[a, b] = keep.tile([P, PASS], U8, name="w1s%d%d" % (a, b), align_bytes=64)
-            nc.vector.quantize_mx(
-                out=w1_q[a, b][:].bitcast(E4M3X4),
-                scales=w1_sc[a, b][:],
-                in_=grouped[a, b][:].rearrange("p t m j -> p (t m j)"),
-            )
+            pieces = PACK if a == K_PASSES - 1 else 1
+            width = PASS // pieces
+            flat = grouped[a, b][:].rearrange("p t m j -> p (t m j)")
+            for u in range(pieces):
+                cols = slice(width * u, width * (u + 1))
+                nc.vector.quantize_mx(
+                    out=w1_q[a, b][:, cols].bitcast(E4M3X4),
+                    scales=w1_sc[a, b][:, cols],
+                    in_=flat[:, PACK * width * u : PACK * width * (u + 1)],
+                )
 
         def gather(a, jh):
             v_w[a, jh] = keep.tile([P, PASS], U32, name="vw%d%d" % (a, jh), align_bytes=64)
@@ -116,25 +162,40 @@ def tile_list_perturbation_program_scores_kernel(
         h_q = {}
         h_sc = {}
 
-        def activate(b, jh):
-            hp = ring.tile([P, PACK, PASS], BF16, name="h_planes", align_bytes=64)
+        def rectify(b, jh, on_scalar):
+            hp = ring.tile([P, PACK, PASS], F32, name="h_planes", align_bytes=64, bufs=4)
             h_planes[b, jh] = hp
             for t in range(PACK):
-                r = ring.tile([P, PASS], F32, name="relu", bufs=4)
-                nc.scalar.activation(out=r[:], in_=acc[b, jh, t][:], func=ACT.Relu)
-                nc.vector.scalar_tensor_tensor(
-                    out=hp[:, t, :], in0=r[:], scalar=gain_sb[:, b, t : t + 1], in1=r[:],
-                    op0=ALU.mult, op1=ALU.mult,
-                )
+                col = root[:, PACK * b + t : PACK * b + t + 1]
+                if t in on_scalar:
+                    nc.scalar.activation(out=hp[:, t, :], in_=acc[b, jh, t][:], func=ACT.Relu, scale=col)
+                else:
+                    nc.vector.tensor_scalar(
+                        out=hp[:, t, :], in0=acc[b, jh, t][:], scalar1=0.0, scalar2=col,
+                        op0=ALU.max, op1=ALU.mult,
+                    )
 
         h_woven = {}
+        h_signed = {}
 
-        def weave(b, jh):
-            hw = ring.tile([P, PASS, PACK], BF16, name="h_woven", align_bytes=64)
+        def square(b, jh):
+            hw = ring.tile([P, PASS, PACK], BF16, name="h_woven", align_bytes=64, bufs=4)
             h_woven[b, jh] = hw
-            nc.vector.tensor_copy(
+            nc.scalar.activation(
                 out=hw[:].rearrange("p (c i) t -> p c t i", i=4),
                 in_=h_planes[b, jh][:].rearrange("p t (c i) -> p c t i", i=4),
+                func=ACT.Square,
+            )
+
+        def apply_sign(b, jh):
+            hs = ring.tile([P, PASS, PACK], BF16, name="to_quantise", align_bytes=64)
+            h_signed[b, jh] = hs
+            reps = PASS // SIGN_COLS
+            nc.vector.tensor_tensor(
+                out=hs[:].rearrange("p (u c) t -> p u (c t)", u=reps),
+                in0=h_woven[b, jh][:].rearrange("p (u c) t -> p u (c t)", u=reps),
+                in1=sign[:, b].rearrange("p c t -> p (c t)").unsqueeze(1).to_broadcast([P, reps, SIGN_COLS * PACK]),
+                op=ALU.mult,
             )
 
         def quant_h(b, jh):
@@ -143,45 +204,31 @@ def tile_list_perturbation_program_scores_kernel(
             nc.vector.quantize_mx(
                 out=h_q[b, jh][:].bitcast(E4M3X4),
                 scales=h_sc[b, jh][:],
-                in_=h_woven[b, jh][:].rearrange("p c t -> p (c t)"),
+                in_=h_signed[b, jh][:].rearrange("p c t -> p (c t)"),
             )
 
         for a in range(K_PASSES):
-            load_w1(a, 0)
+            load_tab(a)
             if a == 2:
                 for a2 in range(1, K_PASSES):
                     nc.sync.dma_start(
                         out=v_sc[a2][0:100, :].bitcast(I32), in_=v_sc[0][4 * a2 : 4 * a2 + 100, :].bitcast(I32)
                     )
-            load_tab(a)
-            cast_w1(a, 0, P)
-            quant_w1(a, 0)
+            load_w1(a, 0)
             for jh in range(J_HALVES):
                 gather(a, jh)
+            cast_w1(a, 0, (P,) if a < K_PASSES - 1 else (64, 24))
+            quant_w1(a, 0)
         for a in range(K_PASSES):
             for jh in range(J_HALVES):
                 stage1(a, 0, jh)
-        nc.sync.dma_start(out=gain_sb[:], in_=gain.rearrange("(b p t) -> p b t", b=R_PASSES, t=PACK))
-        for a in range(K_PASSES):
-            load_w1(a, 1)
-        w2_w = keep.tile([P, R_PASSES, N], U32, name="w2_w", align_bytes=64)
-        nc.sync.dma_start(out=w2_w[:].bitcast(I32), in_=w2_words.rearrange("a p c i -> p a (c i)").bitcast(I32))
-        for q in range(4):
-            nc.sync.dma_start(
-                out=w2_sc[32 * q : 32 * q + 8, :].bitcast(I32),
-                in_=w2_scales[:, 4 * q : 4 * q + 4, :].bitcast(I32),
-            )
-        b2_sb = keep.tile([P, N_TILES], F32, name="b2_sb")
-        with nc.allow_non_contiguous_dma(reason="one bias value a partition"):
-            nc.sync.dma_start(out=b2_sb[:], in_=b2.rearrange("(c p) -> p c", p=P))
-
         def stage2(jh):
-            for c in range(N_TILES):
-                o = psum.tile([P, PASS], F32, name="bank%d" % (4 * jh + c))
-                cols = slice(P * c, P * (c + 1))
-                for b in range(R_PASSES):
+            banks = [psum.tile([P, PASS], F32, name="bank%d" % (4 * jh + c)) for c in range(N_TILES)]
+            for b in range(R_PASSES):
+                for c in range(N_TILES):
+                    cols = slice(P * c, P * (c + 1))
                     nc.tensor.matmul_mx(
-                        out=o[:],
+                        out=banks[c][:],
                         lhsT=w2_w[:, b, cols].bitcast(E4M3X4),
                         lhsT_scale=w2_sc[4 * b : P, cols],
                         rhs=h_q[b, jh][:].bitcast(E4M3X4),
@@ -189,6 +236,9 @@ def tile_list_perturbation_program_scores_kernel(
                         start=(b == 0),
                         stop=(b == R_PASSES - 1),
                     )
+            for c in range(N_TILES):
+                o = banks[c]
+                cols = slice(P * c, P * (c + 1))
                 res = ring.tile([P, PASS], F32, name="res", bufs=8)
                 if jh == 0 or c % 2 == 0:
                     nc.scalar.activation(out=res[:], in_=o[:], func=ACT.Identity, bias=b2_sb[:, c : c + 1])
@@ -198,28 +248,35 @@ def tile_list_perturbation_program_scores_kernel(
                     )
                 nc.sync.dma_start(out=out[cols, PASS * jh : PASS * (jh + 1)], in_=res[:])
 
-        activate(0, 0)
-        cast_w1(0, 1, P)
-        weave(0, 0)
-        quant_w1(0, 1)
-        activate(0, 1)
-        quant_h(0, 0)
-        cast_w1(1, 1, P)
-        weave(0, 1)
-        quant_w1(1, 1)
-        cast_w1(2, 1, P)
-        quant_h(0, 1)
-        quant_w1(2, 1)
-        cast_w1(3, 1, 48)
-        quant_w1(3, 1)
+        rectify(0, 0, range(PACK))
+        rectify(0, 1, range(PACK))
         for a in range(K_PASSES):
+            load_w1(a, 1)
+            cast_w1(a, 1, (0,) if a < K_PASSES - 1 else (0, 0))
+            quant_w1(a, 1)
             for jh in range(J_HALVES):
                 stage1(a, 1, jh)
-        activate(1, 0)
-        weave(1, 0)
-        activate(1, 1)
-        quant_h(1, 0)
-        weave(1, 1)
-        stage2(0)
-        quant_h(1, 1)
-        stage2(1)
+        w2_w = stream_tile([P, R_PASSES, N], U32)
+        nc.sync.dma_start(out=w2_w[:].bitcast(I32), in_=w2_words.rearrange("a p c i -> p a (c i)").bitcast(I32))
+        w2_sc = stream_tile([P, N], U8)
+        nc.vector.memset(w2_sc[:].bitcast(I32), 0)
+        for q in range(4):
+            nc.sync.dma_start(
+                out=w2_sc[32 * q : 32 * q + 8, :].bitcast(I32),
+                in_=w2_scales[:, 4 * q : 4 * q + 4, :].bitcast(I32),
+            )
+        b2_sb = stream_tile([P, N_TILES], F32)
+        with nc.allow_non_contiguous_dma(reason="one bias value a partition"):
+            nc.sync.dma_start(out=b2_sb[:], in_=b2.rearrange("(c p) -> p c", p=P))
+        square(0, 0)
+        square(0, 1)
+        rectify(1, 0, (0, 2))
+        rectify(1, 1, (0, 1, 2))
+        square(1, 0)
+        square(1, 1)
+        for b in range(R_PASSES):
+            for jh in range(J_HALVES):
+                apply_sign(b, jh)
+                quant_h(b, jh)
+        for jh in range(J_HALVES):
+            stage2(jh)

@@ -23,7 +23,14 @@ K_PASSES = K // PASS
 R_PASSES = H // PASS
 J_HALVES = S // PASS
 N_TILES = N // P
+QUAD = 32
+QUADS = P // QUAD
+QUARTER = 256
+J_QUARTERS = S // QUARTER
 SIGN_COLS = 64
+STREAM_BUFS = 4
+CAST_ON_VECTOR = 60
+LAST_CAST_ON_VECTOR = 44
 
 
 def tile_list_perturbation_program_scores_kernel(
@@ -32,58 +39,27 @@ def tile_list_perturbation_program_scores_kernel(
     nc = tc.nc
     with ExitStack() as ctx:
         keep = ctx.enter_context(tc.tile_pool(name="keep", bufs=1))
-        ring = ctx.enter_context(tc.tile_pool(name="ring", bufs=2))
         psum = ctx.enter_context(tc.psum_pool(name="psum", bufs=1))
+
+        streamed = []
+
+        def stream_tile(shape, dtype):
+            tag = "stream%d" % (len(streamed) % STREAM_BUFS)
+            streamed.append(keep.tile(shape, dtype, name=tag, align_bytes=64))
+            return streamed[-1]
 
         offsets = keep.tile([P, S // 16], U16, name="offsets")
         nc.sync.dma_start(offsets[:], offs)
 
         tab_sc = keep.tile([P, T], U8, name="tab_sc", align_bytes=64)
-        nc.gpsimd.memset(tab_sc[:].bitcast(I32), 0)
-        for q in range(4):
-            nc.sync.dma_start(
-                out=tab_sc[32 * q : 32 * q + 16, :].bitcast(I32),
-                in_=tab_scales[:, 4 * q : 4 * q + 4, :].bitcast(I32),
-            )
-        gain_sb = keep.tile([P, R_PASSES * PACK], F32, name="gain_sb")
         nc.sync.dma_start(
-            out=gain_sb[:].rearrange("p (b t) -> p b t", t=PACK),
-            in_=gain.rearrange("(b p t) -> p b t", b=R_PASSES, t=PACK),
+            out=tab_sc[QUAD : 3 * QUAD, :].bitcast(I32),
+            in_=tab_scales.rearrange("a q t -> q a t").bitcast(I32),
         )
-        G = R_PASSES * PACK
-        g_neg = keep.tile([P, G], F32, name="g_neg")
-        g_abs = keep.tile([P, G], F32, name="g_abs")
-        root0 = keep.tile([P, G], F32, name="root0")
-        guard = keep.tile([P, G], F32, name="guard")
-        recip = keep.tile([P, G], F32, name="recip")
-        quot = keep.tile([P, G], F32, name="quot")
-        twice = keep.tile([P, G], F32, name="twice")
-        root = keep.tile([P, G], F32, name="root")
-        nonneg = keep.tile([P, G], F32, name="nonneg")
-        sign = keep.tile([P, R_PASSES, SIGN_COLS, PACK], BF16, name="sign", align_bytes=64)
-        nc.vector.tensor_scalar(out=g_neg[:], in0=gain_sb[:], scalar1=-1.0, scalar2=None, op0=ALU.mult)
-        nc.vector.tensor_scalar(
-            out=nonneg[:], in0=gain_sb[:], scalar1=0.0, scalar2=2.0, op0=ALU.is_ge, op1=ALU.mult
-        )
-        nc.vector.tensor_tensor(out=g_abs[:], in0=gain_sb[:], in1=g_neg[:], op=ALU.max)
-        nc.scalar.activation(out=root0[:], in_=g_abs[:], func=ACT.Sqrt)
-        for b in range(R_PASSES):
-            nc.vector.tensor_scalar(
-                out=sign[:, b],
-                in0=nonneg[:, PACK * b : PACK * (b + 1)].unsqueeze(1).to_broadcast([P, SIGN_COLS, PACK]),
-                scalar1=-1.0, scalar2=None, op0=ALU.add,
-            )
-        nc.vector.tensor_scalar(out=guard[:], in0=root0[:], scalar1=1e-30, scalar2=None, op0=ALU.max)
-        nc.vector.reciprocal(out=recip[:], in_=guard[:])
-        nc.vector.tensor_tensor(out=quot[:], in0=g_abs[:], in1=recip[:], op=ALU.mult)
-        nc.vector.tensor_tensor(out=twice[:], in0=quot[:], in1=root0[:], op=ALU.add)
-        nc.vector.tensor_scalar(out=root[:], in0=twice[:], scalar1=0.5, scalar2=None, op0=ALU.mult)
-
-        v_sc = [keep.tile([P, S], U8, name="v_sc%d" % a, align_bytes=64) for a in range(K_PASSES)]
-        for a in range(1, K_PASSES):
-            nc.vector.memset(v_sc[a][:].bitcast(I32), 0)
-
-        nc.vector.tensor_copy(v_sc[0][:], tab_sc[:].indirect(offsets[:]))
+        nc.gpsimd.memset(tab_sc[0:QUAD, :].bitcast(I32), 0)
+        nc.gpsimd.memset(tab_sc[3 * QUAD : P, :].bitcast(I32), 0)
+        v_sc = keep.tile([P, K_PASSES, S], U8, name="v_sc", align_bytes=64)
+        nc.gpsimd.memset(v_sc[:].rearrange("p a j -> p (a j)").bitcast(I32), 0)
 
         raw = {}
         tabw = {}
@@ -92,8 +68,9 @@ def tile_list_perturbation_program_scores_kernel(
         v_w = {}
         grouped = {}
 
-        def stream_tile(shape, dtype):
-            return ring.tile(shape, dtype, name="stream", align_bytes=64, bufs=5)
+        def load_tab(a):
+            tabw[a] = stream_tile([P, T], U32)
+            nc.sync.dma_start(out=tabw[a][:].bitcast(I32), in_=tab_words[a].rearrange("p t i -> p (t i)").bitcast(I32))
 
         def load_w1(a, b):
             pieces = 2 if a == K_PASSES - 1 else 1
@@ -105,21 +82,63 @@ def tile_list_perturbation_program_scores_kernel(
                 src = w1[PASS * a : PASS * (a + 1), c0 : c0 + width]
                 nc.sync.dma_start(out=raw[a, b, u], in_=src.rearrange("(p j) c -> p j c", j=PACK))
 
-        def load_tab(a):
-            tabw[a] = stream_tile([P, T], U32)
-            nc.sync.dma_start(out=tabw[a][:].bitcast(I32), in_=tab_words[a].rearrange("p t i -> p (t i)").bitcast(I32))
+        load_tab(0)
+        gain_sb = keep.tile([P, R_PASSES * PACK], F32, name="gain_sb")
+        nc.sync.dma_start(
+            out=gain_sb[:].rearrange("p (b t) -> p b t", t=PACK),
+            in_=gain.rearrange("(b p t) -> p b t", b=R_PASSES, t=PACK),
+        )
 
-        def cast_w1(a, b, on_scalar):
-            g = ring.tile([P, PACK, P, PACK], BF16, name="to_quantise", align_bytes=64)
+        picked_sc = keep.tile([P, S], U8, name="picked_sc", align_bytes=64)
+        nc.vector.tensor_copy(picked_sc[:], tab_sc[:].indirect(offsets[:]))
+        for q in range(QUADS):
+            nc.scalar.dma_start(
+                out=v_sc[QUAD * q : QUAD * q + 4].bitcast(I32),
+                in_=picked_sc[QUAD + 16 * q : QUAD + 16 * (q + 1), :].bitcast(I32),
+            )
+
+        G = R_PASSES * PACK
+        g_neg = keep.tile([P, G], F32, name="g_neg")
+        g_abs = keep.tile([P, G], F32, name="g_abs")
+        root0 = keep.tile([P, G], F32, name="root0")
+        guard = keep.tile([P, G], F32, name="guard")
+        recip = keep.tile([P, G], F32, name="recip")
+        quot = keep.tile([P, G], F32, name="quot")
+        twice = keep.tile([P, G], F32, name="twice")
+        root = keep.tile([P, G], F32, name="root")
+        nonneg = keep.tile([P, G], F32, name="nonneg")
+        sign = keep.tile([P, R_PASSES, SIGN_COLS, PACK], BF16, name="sign", align_bytes=64)
+
+        def split_gain():
+            nc.vector.tensor_scalar(out=g_neg[:], in0=gain_sb[:], scalar1=-1.0, scalar2=None, op0=ALU.mult)
+            nc.vector.tensor_scalar(
+                out=nonneg[:], in0=gain_sb[:], scalar1=0.0, scalar2=2.0, op0=ALU.is_ge, op1=ALU.mult
+            )
+            nc.vector.tensor_tensor(out=g_abs[:], in0=gain_sb[:], in1=g_neg[:], op=ALU.max)
+            nc.scalar.activation(out=root0[:], in_=g_abs[:], func=ACT.Sqrt)
+            for b in range(R_PASSES):
+                nc.vector.tensor_scalar(
+                    out=sign[:, b],
+                    in0=nonneg[:, PACK * b : PACK * (b + 1)].unsqueeze(1).to_broadcast([P, SIGN_COLS, PACK]),
+                    scalar1=-1.0, scalar2=None, op0=ALU.add,
+                )
+            nc.vector.tensor_scalar(out=guard[:], in0=root0[:], scalar1=1e-30, scalar2=None, op0=ALU.max)
+            nc.vector.reciprocal(out=recip[:], in_=guard[:])
+            nc.vector.tensor_tensor(out=quot[:], in0=g_abs[:], in1=recip[:], op=ALU.mult)
+            nc.vector.tensor_tensor(out=twice[:], in0=quot[:], in1=root0[:], op=ALU.add)
+            nc.vector.tensor_scalar(out=root[:], in0=twice[:], scalar1=0.5, scalar2=None, op0=ALU.mult)
+
+        def cast_w1(a, b, on_vector):
+            g = keep.tile([P, PACK, P, PACK], BF16, name="grouped%d" % (a % 2), align_bytes=64)
             grouped[a, b] = g
-            groups = P // len(on_scalar)
-            for u, split in enumerate(on_scalar):
+            groups = P // len(on_vector)
+            for u, split in enumerate(on_vector):
                 dst = g[:].rearrange("p t m j -> p m t j")[:, groups * u : groups * (u + 1)]
                 src = raw[a, b, u].rearrange("p j (m t) -> p m t j", t=PACK)
                 if split > 0:
-                    nc.scalar.activation(out=dst[:, 0:split], in_=src[:, 0:split], func=ACT.Copy)
+                    nc.vector.tensor_copy(out=dst[:, 0:split], in_=src[:, 0:split])
                 if split < groups:
-                    nc.vector.tensor_copy(out=dst[:, split:groups], in_=src[:, split:groups])
+                    nc.scalar.activation(out=dst[:, split:groups], in_=src[:, split:groups], func=ACT.Copy)
 
         def quant_w1(a, b):
             w1_q[a, b] = keep.tile([P, PASS], U32, name="w1q%d%d" % (a, b), align_bytes=64)
@@ -137,146 +156,162 @@ def tile_list_perturbation_program_scores_kernel(
 
         def gather(a, jh):
             v_w[a, jh] = keep.tile([P, PASS], U32, name="vw%d%d" % (a, jh), align_bytes=64)
-            nc.vector.tensor_copy(
-                v_w[a, jh][:], tabw[a][:].indirect(offsets[:, 32 * jh : 32 * (jh + 1)])
-            )
+            nc.vector.tensor_copy(v_w[a, jh][:], tabw[a][:].indirect(offsets[:, 32 * jh : 32 * (jh + 1)]))
 
         acc = {}
 
         def stage1(a, b, jh):
             for t in range(PACK):
                 if a == 0:
-                    acc[b, jh, t] = psum.tile([P, PASS], F32, name="bank%d" % (4 * jh + t))
+                    acc[b, jh, t] = psum.tile([P, PASS], F32, name="bank%d" % (PACK * jh + t))
                 cols = slice(P * t, P * (t + 1))
                 nc.tensor.matmul_mx(
                     out=acc[b, jh, t][:],
                     lhsT=w1_q[a, b][:, cols].bitcast(E4M3X4),
                     lhsT_scale=w1_sc[a, b][:, cols],
                     rhs=v_w[a, jh][:].bitcast(E5M2X4),
-                    rhs_scale=v_sc[a][:, PASS * jh : PASS * (jh + 1)],
+                    rhs_scale=v_sc[:, a, PASS * jh : PASS * (jh + 1)],
                     start=(a == 0),
                     stop=(a == K_PASSES - 1),
                 )
 
-        h_planes = {}
+        planes = {}
+        woven = {}
         h_q = {}
         h_sc = {}
 
-        def rectify(b, jh, on_scalar):
-            hp = ring.tile([P, PACK, PASS], F32, name="h_planes", align_bytes=64, bufs=4)
-            h_planes[b, jh] = hp
+        def rectify(b, jh, on_vector):
+            planes[b, jh] = keep.tile([P, PACK, PASS], F32, name="planes%d%d" % (b, jh), align_bytes=64)
             for t in range(PACK):
                 col = root[:, PACK * b + t : PACK * b + t + 1]
-                if t in on_scalar:
-                    nc.scalar.activation(out=hp[:, t, :], in_=acc[b, jh, t][:], func=ACT.Relu, scale=col)
-                else:
+                if t in on_vector:
                     nc.vector.tensor_scalar(
-                        out=hp[:, t, :], in0=acc[b, jh, t][:], scalar1=0.0, scalar2=col,
+                        out=planes[b, jh][:, t, :], in0=acc[b, jh, t][:], scalar1=0.0, scalar2=col,
                         op0=ALU.max, op1=ALU.mult,
                     )
+                else:
+                    nc.scalar.activation(out=planes[b, jh][:, t, :], in_=acc[b, jh, t][:], func=ACT.Relu, scale=col)
 
-        h_woven = {}
-        h_signed = {}
-
-        def square(b, jh):
-            hw = ring.tile([P, PASS, PACK], BF16, name="h_woven", align_bytes=64, bufs=4)
-            h_woven[b, jh] = hw
+        def square(b, jq):
+            woven[b, jq] = keep.tile([P, QUARTER, PACK], BF16, name="woven%d%d" % (b, jq), align_bytes=64)
+            c0 = QUARTER * (jq % 2)
             nc.scalar.activation(
-                out=hw[:].rearrange("p (c i) t -> p c t i", i=4),
-                in_=h_planes[b, jh][:].rearrange("p t (c i) -> p c t i", i=4),
+                out=woven[b, jq][:].rearrange("p (c i) t -> p c t i", i=4),
+                in_=planes[b, jq // 2][:, :, c0 : c0 + QUARTER].rearrange("p t (c i) -> p c t i", i=4),
                 func=ACT.Square,
             )
 
-        def apply_sign(b, jh):
-            hs = ring.tile([P, PASS, PACK], BF16, name="to_quantise", align_bytes=64)
-            h_signed[b, jh] = hs
-            reps = PASS // SIGN_COLS
+        signed = {}
+
+        def apply_sign(b, jq):
+            signed[b, jq] = keep.tile([P, QUARTER, PACK], BF16, name="signed%d" % (jq % 2), align_bytes=64)
+            reps = QUARTER // SIGN_COLS
             nc.vector.tensor_tensor(
-                out=hs[:].rearrange("p (u c) t -> p u (c t)", u=reps),
-                in0=h_woven[b, jh][:].rearrange("p (u c) t -> p u (c t)", u=reps),
+                out=signed[b, jq][:].rearrange("p (u c) t -> p u (c t)", u=reps),
+                in0=woven[b, jq][:].rearrange("p (u c) t -> p u (c t)", u=reps),
                 in1=sign[:, b].rearrange("p c t -> p (c t)").unsqueeze(1).to_broadcast([P, reps, SIGN_COLS * PACK]),
                 op=ALU.mult,
             )
 
-        def quant_h(b, jh):
-            h_q[b, jh] = keep.tile([P, PASS], U32, name="hq%d%d" % (b, jh), align_bytes=64)
-            h_sc[b, jh] = keep.tile([P, PASS], U8, name="hs%d%d" % (b, jh), align_bytes=64)
+        def quant_h(b, jq):
+            h_q[b, jq] = keep.tile([P, QUARTER], U32, name="hq%d%d" % (b, jq), align_bytes=64)
+            h_sc[b, jq] = keep.tile([P, QUARTER], U8, name="hs%d%d" % (b, jq), align_bytes=64)
             nc.vector.quantize_mx(
-                out=h_q[b, jh][:].bitcast(E4M3X4),
-                scales=h_sc[b, jh][:],
-                in_=h_signed[b, jh][:].rearrange("p c t -> p (c t)"),
+                out=h_q[b, jq][:].bitcast(E4M3X4),
+                scales=h_sc[b, jq][:],
+                in_=signed[b, jq][:].rearrange("p c t -> p (c t)"),
             )
 
-        for a in range(K_PASSES):
-            load_tab(a)
-            if a == 2:
-                for a2 in range(1, K_PASSES):
-                    nc.sync.dma_start(
-                        out=v_sc[a2][0:100, :].bitcast(I32), in_=v_sc[0][4 * a2 : 4 * a2 + 100, :].bitcast(I32)
-                    )
-            load_w1(a, 0)
-            for jh in range(J_HALVES):
-                gather(a, jh)
-            cast_w1(a, 0, (P,) if a < K_PASSES - 1 else (64, 24))
-            quant_w1(a, 0)
-        for a in range(K_PASSES):
-            for jh in range(J_HALVES):
-                stage1(a, 0, jh)
-        def stage2(jh):
-            banks = [psum.tile([P, PASS], F32, name="bank%d" % (4 * jh + c)) for c in range(N_TILES)]
+        def stage2(jq, on_vector):
+            banks = [
+                psum.tile([P, 2, QUARTER], F32, name="bank%d" % (2 * jq + pair)) for pair in range(N_TILES // 2)
+            ]
             for b in range(R_PASSES):
                 for c in range(N_TILES):
                     cols = slice(P * c, P * (c + 1))
                     nc.tensor.matmul_mx(
-                        out=banks[c][:],
+                        out=banks[c // 2][:, c % 2, :],
                         lhsT=w2_w[:, b, cols].bitcast(E4M3X4),
                         lhsT_scale=w2_sc[4 * b : P, cols],
-                        rhs=h_q[b, jh][:].bitcast(E4M3X4),
-                        rhs_scale=h_sc[b, jh][:],
-                        start=(b == 0),
-                        stop=(b == R_PASSES - 1),
+                        rhs=h_q[b, jq][:].bitcast(E4M3X4),
+                        rhs_scale=h_sc[b, jq][:],
+                        start=(b == 0 and c % 2 == 0),
+                        stop=(b == R_PASSES - 1 and c % 2 == 1),
                     )
-            for c in range(N_TILES):
-                o = banks[c]
-                cols = slice(P * c, P * (c + 1))
-                res = ring.tile([P, PASS], F32, name="res", bufs=8)
-                if jh == 0 or c % 2 == 0:
-                    nc.scalar.activation(out=res[:], in_=o[:], func=ACT.Identity, bias=b2_sb[:, c : c + 1])
-                else:
-                    nc.vector.tensor_scalar(
-                        out=res[:], in0=o[:], scalar1=b2_sb[:, c : c + 1], scalar2=None, op0=ALU.add
-                    )
-                nc.sync.dma_start(out=out[cols, PASS * jh : PASS * (jh + 1)], in_=res[:])
+            for pair in range(N_TILES // 2):
+                res = keep.tile([P, 2, QUARTER], F32, name="res%d%d" % (jq, pair))
+                for half in range(2):
+                    c = 2 * pair + half
+                    if pair in on_vector:
+                        nc.vector.tensor_scalar(
+                            out=res[:, half, :], in0=banks[pair][:, half, :], scalar1=b2_sb[:, c : c + 1],
+                            scalar2=None, op0=ALU.add,
+                        )
+                    else:
+                        nc.scalar.activation(
+                            out=res[:, half, :], in_=banks[pair][:, half, :], func=ACT.Identity,
+                            bias=b2_sb[:, c : c + 1],
+                        )
+                rows = out[2 * P * pair : 2 * P * (pair + 1), QUARTER * jq : QUARTER * (jq + 1)]
+                nc.sync.dma_start(out=rows.rearrange("(c p) j -> p c j", p=P), in_=res[:])
 
-        rectify(0, 0, range(PACK))
-        rectify(0, 1, range(PACK))
+        last = K_PASSES - 1
+        for a in range(K_PASSES):
+            if a > 0:
+                load_tab(a)
+            load_w1(a, 0)
+            for jh in range(J_HALVES):
+                gather(a, jh)
+            if a == 0:
+                split_gain()
+            cast_w1(a, 0, (CAST_ON_VECTOR,) if a < last else (0, LAST_CAST_ON_VECTOR))
+            quant_w1(a, 0)
+            for jh in range(J_HALVES):
+                stage1(a, 0, jh)
+
+        rectify(0, 0, (1,))
+        rectify(0, 1, ())
         for a in range(K_PASSES):
             load_w1(a, 1)
-            cast_w1(a, 1, (0,) if a < K_PASSES - 1 else (0, 0))
+            cast_w1(a, 1, (P,) if a < last else (P // 2, P // 2))
             quant_w1(a, 1)
-            for jh in range(J_HALVES):
-                stage1(a, 1, jh)
+            if a < last - 1:
+                for jh in range(J_HALVES):
+                    stage1(a, 1, jh)
+        for jh in range(J_HALVES):
+            stage1(last - 1, 1, jh)
+            stage1(last, 1, jh)
+
         w2_w = stream_tile([P, R_PASSES, N], U32)
         nc.sync.dma_start(out=w2_w[:].bitcast(I32), in_=w2_words.rearrange("a p c i -> p a (c i)").bitcast(I32))
         w2_sc = stream_tile([P, N], U8)
-        nc.vector.memset(w2_sc[:].bitcast(I32), 0)
-        for q in range(4):
+        nc.gpsimd.memset(w2_sc[:].bitcast(I32), 0)
+        for q in range(QUADS):
             nc.sync.dma_start(
-                out=w2_sc[32 * q : 32 * q + 8, :].bitcast(I32),
+                out=w2_sc[QUAD * q : QUAD * q + 8, :].bitcast(I32),
                 in_=w2_scales[:, 4 * q : 4 * q + 4, :].bitcast(I32),
             )
         b2_sb = stream_tile([P, N_TILES], F32)
         with nc.allow_non_contiguous_dma(reason="one bias value a partition"):
             nc.sync.dma_start(out=b2_sb[:], in_=b2.rearrange("(c p) -> p c", p=P))
-        square(0, 0)
-        square(0, 1)
-        rectify(1, 0, (0, 2))
+
+        for jq in range(J_QUARTERS):
+            square(0, jq)
+        rectify(1, 0, (1, 3))
+        for jq in range(2):
+            apply_sign(0, jq)
+            quant_h(0, jq)
+        for jq in range(2):
+            square(1, jq)
+            apply_sign(1, jq)
+            quant_h(1, jq)
         rectify(1, 1, (0, 1, 2))
-        square(1, 0)
-        square(1, 1)
-        for b in range(R_PASSES):
-            for jh in range(J_HALVES):
-                apply_sign(b, jh)
-                quant_h(b, jh)
-        for jh in range(J_HALVES):
-            stage2(jh)
+        for jq in range(2, J_QUARTERS):
+            square(1, jq)
+        for jq in range(2):
+            stage2(jq, ())
+        for jq in range(2, J_QUARTERS):
+            for b in range(R_PASSES):
+                apply_sign(b, jq)
+                quant_h(b, jq)
+            stage2(jq, (1,) if jq == J_QUARTERS - 1 else ())

@@ -133,17 +133,19 @@ def tile_list_perturbation_program_scores_kernel(
             grouped[a, b] = g
             groups = P // len(on_vector)
             for u, split in enumerate(on_vector):
-                dst = g[:].rearrange("p t m j -> p m t j")[:, groups * u : groups * (u + 1)]
-                src = raw[a, b, u].rearrange("p j (m t) -> p m t j", t=PACK)
-                if split > 0:
-                    nc.vector.tensor_copy(out=dst[:, 0:split], in_=src[:, 0:split])
-                if split < groups:
-                    nc.scalar.activation(out=dst[:, split:groups], in_=src[:, split:groups], func=ACT.Copy)
+                for pair in range(PACK // 2):
+                    ts = slice(2 * pair, 2 * pair + 2)
+                    dst = g[:, ts].rearrange("p t m j -> p m j t")[:, groups * u : groups * (u + 1)]
+                    src = raw[a, b, u].rearrange("p j (m t) -> p m j t", t=PACK)[:, :, :, ts]
+                    if split > 0:
+                        nc.vector.tensor_copy(out=dst[:, 0:split], in_=src[:, 0:split])
+                    if split < groups:
+                        nc.scalar.activation(out=dst[:, split:groups], in_=src[:, split:groups], func=ACT.Copy)
 
         def quant_w1(a, b):
             w1_q[a, b] = keep.tile([P, PASS], U32, name="w1q%d%d" % (a, b), align_bytes=64)
             w1_sc[a, b] = keep.tile([P, PASS], U8, name="w1s%d%d" % (a, b), align_bytes=64)
-            pieces = PACK if a == K_PASSES - 1 else 1
+            pieces = 2
             width = PASS // pieces
             flat = grouped[a, b][:].rearrange("p t m j -> p (t m j)")
             for u in range(pieces):

@@ -29,8 +29,8 @@ QUARTER = 256
 J_QUARTERS = S // QUARTER
 SIGN_COLS = 64
 STREAM_BUFS = 4
-CAST_ON_VECTOR = 60
-LAST_CAST_ON_VECTOR = 44
+CAST_ON_VECTOR = 64
+LAST_CAST_ON_VECTOR = 42
 
 
 def tile_list_perturbation_program_scores_kernel(
@@ -51,7 +51,7 @@ def tile_list_perturbation_program_scores_kernel(
         offsets = keep.tile([P, S // 16], U16, name="offsets")
         nc.sync.dma_start(offsets[:], offs)
 
-        tab_sc = keep.tile([P, T], U8, name="tab_sc", align_bytes=64)
+        tab_sc = stream_tile([P, T], U8)
         nc.sync.dma_start(
             out=tab_sc[QUAD : 3 * QUAD, :].bitcast(I32),
             in_=tab_scales.rearrange("a q t -> q a t").bitcast(I32),
@@ -89,10 +89,12 @@ def tile_list_perturbation_program_scores_kernel(
             in_=gain.rearrange("(b p t) -> p b t", b=R_PASSES, t=PACK),
         )
 
+        load_w1(0, 0)
+        load_tab(1)
         picked_sc = keep.tile([P, S], U8, name="picked_sc", align_bytes=64)
         nc.vector.tensor_copy(picked_sc[:], tab_sc[:].indirect(offsets[:]))
         for q in range(QUADS):
-            nc.scalar.dma_start(
+            nc.sync.dma_start(
                 out=v_sc[QUAD * q : QUAD * q + 4].bitcast(I32),
                 in_=picked_sc[QUAD + 16 * q : QUAD + 16 * (q + 1), :].bitcast(I32),
             )
@@ -205,8 +207,8 @@ def tile_list_perturbation_program_scores_kernel(
 
         signed = {}
 
-        def apply_sign(b, jq):
-            signed[b, jq] = keep.tile([P, QUARTER, PACK], BF16, name="signed%d" % (jq % 2), align_bytes=64)
+        def apply_sign(b, jq, tag):
+            signed[b, jq] = keep.tile([P, QUARTER, PACK], BF16, name=tag, align_bytes=64)
             reps = QUARTER // SIGN_COLS
             nc.vector.tensor_tensor(
                 out=signed[b, jq][:].rearrange("p (u c) t -> p u (c t)", u=reps),
@@ -258,10 +260,12 @@ def tile_list_perturbation_program_scores_kernel(
                 nc.sync.dma_start(out=rows.rearrange("(c p) j -> p c j", p=P), in_=res[:])
 
         last = K_PASSES - 1
+        load_w1(1, 0)
+        load_tab(2)
+        load_w1(2, 0)
+        load_tab(3)
+        load_w1(3, 0)
         for a in range(K_PASSES):
-            if a > 0:
-                load_tab(a)
-            load_w1(a, 0)
             for jh in range(J_HALVES):
                 gather(a, jh)
             if a == 0:
@@ -300,20 +304,27 @@ def tile_list_perturbation_program_scores_kernel(
         for jq in range(J_QUARTERS):
             square(0, jq)
         rectify(1, 0, (1, 3))
-        for jq in range(2):
-            apply_sign(0, jq)
-            quant_h(0, jq)
-        for jq in range(2):
+        apply_sign(0, 0, "signed0")
+        quant_h(0, 0)
+        square(1, 0)
+        apply_sign(0, 1, "grouped1")
+        rectify(1, 1, (1, 3))
+        quant_h(0, 1)
+        square(1, 1)
+        apply_sign(1, 0, "signed0")
+        quant_h(1, 0)
+        apply_sign(1, 1, "signed1")
+        quant_h(1, 1)
+        stage2(0, ())
+        for jq in range(2, J_QUARTERS):
             square(1, jq)
-            apply_sign(1, jq)
+        stage2(1, ())
+        apply_sign(0, 2, "grouped1")
+        apply_sign(0, 3, "signed0")
+        quant_h(0, 2)
+        quant_h(0, 3)
+        for jq in range(2, J_QUARTERS):
+            apply_sign(1, jq, "signed%d" % (jq % 2))
             quant_h(1, jq)
-        rectify(1, 1, (0, 1, 2))
         for jq in range(2, J_QUARTERS):
-            square(1, jq)
-        for jq in range(2):
-            stage2(jq, ())
-        for jq in range(2, J_QUARTERS):
-            for b in range(R_PASSES):
-                apply_sign(b, jq)
-                quant_h(b, jq)
-            stage2(jq, (1,) if jq == J_QUARTERS - 1 else ())
+            stage2(jq, (1,))

@@ -28,9 +28,9 @@ QUADS = P // QUAD
 QUARTER = 256
 J_QUARTERS = S // QUARTER
 SIGN_COLS = 64
+BLOCK_WORDS = 8
 STREAM_BUFS = 4
-CAST_ON_VECTOR = 64
-LAST_CAST_ON_VECTOR = 42
+BLOCK0_CASTS_ON_VECTOR = ((0,), (0,), (64,), (0, 42))
 
 
 def tile_list_perturbation_program_scores_kernel(
@@ -60,6 +60,13 @@ def tile_list_perturbation_program_scores_kernel(
         nc.gpsimd.memset(tab_sc[3 * QUAD : P, :].bitcast(I32), 0)
         v_sc = keep.tile([P, K_PASSES, S], U8, name="v_sc", align_bytes=64)
         nc.gpsimd.memset(v_sc[:].rearrange("p a j -> p (a j)").bitcast(I32), 0)
+        w2_sc = keep.tile([P, N], U8, name="w2_sc", align_bytes=64)
+        nc.gpsimd.memset(w2_sc[:].bitcast(I32), 0)
+        for q in range(QUADS):
+            nc.gpsimd.dma_start(
+                out=w2_sc[QUAD * q : QUAD * q + 8, :].bitcast(I32),
+                in_=w2_scales[:, 4 * q : 4 * q + 4, :].bitcast(I32),
+            )
 
         raw = {}
         tabw = {}
@@ -83,11 +90,9 @@ def tile_list_perturbation_program_scores_kernel(
                 nc.sync.dma_start(out=raw[a, b, u], in_=src.rearrange("(p j) c -> p j c", j=PACK))
 
         load_tab(0)
-        gain_sb = keep.tile([P, R_PASSES * PACK], F32, name="gain_sb")
-        nc.sync.dma_start(
-            out=gain_sb[:].rearrange("p (b t) -> p b t", t=PACK),
-            in_=gain.rearrange("(b p t) -> p b t", b=R_PASSES, t=PACK),
-        )
+        gain_rows = keep.tile([P, R_PASSES, BLOCK_WORDS], F32, name="gain_rows")
+        gain_sb = gain_rows[:, :, 0:PACK]
+        nc.sync.dma_start(out=gain_sb, in_=gain.rearrange("(b p t) -> p b t", b=R_PASSES, t=PACK))
 
         load_w1(0, 0)
         load_tab(1)
@@ -100,7 +105,6 @@ def tile_list_perturbation_program_scores_kernel(
             )
 
         G = R_PASSES * PACK
-        g_neg = keep.tile([P, G], F32, name="g_neg")
         g_abs = keep.tile([P, G], F32, name="g_abs")
         root0 = keep.tile([P, G], F32, name="root0")
         guard = keep.tile([P, G], F32, name="guard")
@@ -108,27 +112,19 @@ def tile_list_perturbation_program_scores_kernel(
         quot = keep.tile([P, G], F32, name="quot")
         twice = keep.tile([P, G], F32, name="twice")
         root = keep.tile([P, G], F32, name="root")
-        nonneg = keep.tile([P, G], F32, name="nonneg")
         sign = keep.tile([P, R_PASSES, SIGN_COLS, PACK], BF16, name="sign", align_bytes=64)
 
         def split_gain():
-            nc.vector.tensor_scalar(out=g_neg[:], in0=gain_sb[:], scalar1=-1.0, scalar2=None, op0=ALU.mult)
-            nc.vector.tensor_scalar(
-                out=nonneg[:], in0=gain_sb[:], scalar1=0.0, scalar2=2.0, op0=ALU.is_ge, op1=ALU.mult
-            )
-            nc.vector.tensor_tensor(out=g_abs[:], in0=gain_sb[:], in1=g_neg[:], op=ALU.max)
+            nc.scalar.activation(out=g_abs[:].rearrange("p (b t) -> p b t", t=PACK), in_=gain_sb, func=ACT.Abs)
             nc.scalar.activation(out=root0[:], in_=g_abs[:], func=ACT.Sqrt)
-            for b in range(R_PASSES):
-                nc.vector.tensor_scalar(
-                    out=sign[:, b],
-                    in0=nonneg[:, PACK * b : PACK * (b + 1)].unsqueeze(1).to_broadcast([P, SIGN_COLS, PACK]),
-                    scalar1=-1.0, scalar2=None, op0=ALU.add,
-                )
-            nc.vector.tensor_scalar(out=guard[:], in0=root0[:], scalar1=1e-30, scalar2=None, op0=ALU.max)
+            nc.scalar.activation(
+                out=sign[:], in_=gain_sb.unsqueeze(2).to_broadcast([P, R_PASSES, SIGN_COLS, PACK]), func=ACT.Sign
+            )
+            nc.gpsimd.tensor_scalar(out=guard[:], in0=root0[:], scalar1=1e-30, scalar2=None, op0=ALU.max)
             nc.vector.reciprocal(out=recip[:], in_=guard[:])
-            nc.vector.tensor_tensor(out=quot[:], in0=g_abs[:], in1=recip[:], op=ALU.mult)
-            nc.vector.tensor_tensor(out=twice[:], in0=quot[:], in1=root0[:], op=ALU.add)
-            nc.vector.tensor_scalar(out=root[:], in0=twice[:], scalar1=0.5, scalar2=None, op0=ALU.mult)
+            nc.gpsimd.tensor_tensor(out=quot[:], in0=g_abs[:], in1=recip[:], op=ALU.mult)
+            nc.gpsimd.tensor_tensor(out=twice[:], in0=quot[:], in1=root0[:], op=ALU.add)
+            nc.gpsimd.tensor_scalar(out=root[:], in0=twice[:], scalar1=0.5, scalar2=None, op0=ALU.mult)
 
         def cast_w1(a, b, on_vector):
             g = keep.tile([P, PACK, P, PACK], BF16, name="grouped%d" % (a % 2), align_bytes=64)
@@ -184,17 +180,17 @@ def tile_list_perturbation_program_scores_kernel(
         h_q = {}
         h_sc = {}
 
-        def rectify(b, jh, on_vector):
-            planes[b, jh] = keep.tile([P, PACK, PASS], F32, name="planes%d%d" % (b, jh), align_bytes=64)
-            for t in range(PACK):
-                col = root[:, PACK * b + t : PACK * b + t + 1]
-                if t in on_vector:
-                    nc.vector.tensor_scalar(
-                        out=planes[b, jh][:, t, :], in0=acc[b, jh, t][:], scalar1=0.0, scalar2=col,
-                        op0=ALU.max, op1=ALU.mult,
-                    )
-                else:
-                    nc.scalar.activation(out=planes[b, jh][:, t, :], in_=acc[b, jh, t][:], func=ACT.Relu, scale=col)
+        def rectify(b, jh, t, on_vector):
+            if (b, jh) not in planes:
+                planes[b, jh] = keep.tile([P, PACK, PASS], F32, name="planes%d%d" % (b, jh), align_bytes=64)
+            col = root[:, PACK * b + t : PACK * b + t + 1]
+            if on_vector:
+                nc.vector.tensor_scalar(
+                    out=planes[b, jh][:, t, :], in0=acc[b, jh, t][:], scalar1=0.0, scalar2=col,
+                    op0=ALU.max, op1=ALU.mult,
+                )
+            else:
+                nc.scalar.activation(out=planes[b, jh][:, t, :], in_=acc[b, jh, t][:], func=ACT.Relu, scale=col)
 
         def square(b, jq):
             woven[b, jq] = keep.tile([P, QUARTER, PACK], BF16, name="woven%d%d" % (b, jq), align_bytes=64)
@@ -207,11 +203,11 @@ def tile_list_perturbation_program_scores_kernel(
 
         signed = {}
 
-        def apply_sign(b, jq, tag):
-            signed[b, jq] = keep.tile([P, QUARTER, PACK], BF16, name=tag, align_bytes=64)
+        def apply_sign(b, jq, staging):
+            signed[b, jq] = staging
             reps = QUARTER // SIGN_COLS
             nc.vector.tensor_tensor(
-                out=signed[b, jq][:].rearrange("p (u c) t -> p u (c t)", u=reps),
+                out=signed[b, jq].rearrange("p (u c) t -> p u (c t)", u=reps),
                 in0=woven[b, jq][:].rearrange("p (u c) t -> p u (c t)", u=reps),
                 in1=sign[:, b].rearrange("p c t -> p (c t)").unsqueeze(1).to_broadcast([P, reps, SIGN_COLS * PACK]),
                 op=ALU.mult,
@@ -223,7 +219,7 @@ def tile_list_perturbation_program_scores_kernel(
             nc.vector.quantize_mx(
                 out=h_q[b, jq][:].bitcast(E4M3X4),
                 scales=h_sc[b, jq][:],
-                in_=signed[b, jq][:].rearrange("p c t -> p (c t)"),
+                in_=signed[b, jq].rearrange("p c t -> p (c t)"),
             )
 
         def stage2(jq, on_vector):
@@ -248,13 +244,13 @@ def tile_list_perturbation_program_scores_kernel(
                     c = 2 * pair + half
                     if pair in on_vector:
                         nc.vector.tensor_scalar(
-                            out=res[:, half, :], in0=banks[pair][:, half, :], scalar1=b2_sb[:, c : c + 1],
+                            out=res[:, half, :], in0=banks[pair][:, half, :], scalar1=b2_rows[:, c, 0:1],
                             scalar2=None, op0=ALU.add,
                         )
                     else:
                         nc.scalar.activation(
                             out=res[:, half, :], in_=banks[pair][:, half, :], func=ACT.Identity,
-                            bias=b2_sb[:, c : c + 1],
+                            bias=b2_rows[:, c, 0:1],
                         )
                 rows = out[2 * P * pair : 2 * P * (pair + 1), QUARTER * jq : QUARTER * (jq + 1)]
                 nc.sync.dma_start(out=rows.rearrange("(c p) j -> p c j", p=P), in_=res[:])
@@ -270,13 +266,14 @@ def tile_list_perturbation_program_scores_kernel(
                 gather(a, jh)
             if a == 0:
                 split_gain()
-            cast_w1(a, 0, (CAST_ON_VECTOR,) if a < last else (0, LAST_CAST_ON_VECTOR))
+            cast_w1(a, 0, BLOCK0_CASTS_ON_VECTOR[a])
             quant_w1(a, 0)
             for jh in range(J_HALVES):
                 stage1(a, 0, jh)
 
-        rectify(0, 0, (1,))
-        rectify(0, 1, ())
+        for jh in range(J_HALVES):
+            for t in range(PACK):
+                rectify(0, jh, t, (jh, t) == (0, 1))
         for a in range(K_PASSES):
             load_w1(a, 1)
             cast_w1(a, 1, (P,) if a < last else (P // 2, P // 2))
@@ -290,41 +287,42 @@ def tile_list_perturbation_program_scores_kernel(
 
         w2_w = stream_tile([P, R_PASSES, N], U32)
         nc.sync.dma_start(out=w2_w[:].bitcast(I32), in_=w2_words.rearrange("a p c i -> p a (c i)").bitcast(I32))
-        w2_sc = stream_tile([P, N], U8)
-        nc.gpsimd.memset(w2_sc[:].bitcast(I32), 0)
-        for q in range(QUADS):
-            nc.sync.dma_start(
-                out=w2_sc[QUAD * q : QUAD * q + 8, :].bitcast(I32),
-                in_=w2_scales[:, 4 * q : 4 * q + 4, :].bitcast(I32),
-            )
-        b2_sb = stream_tile([P, N_TILES], F32)
+        b2_rows = stream_tile([P, N_TILES, BLOCK_WORDS], F32)
+        b2_sb = b2_rows[:, :, 0]
         with nc.allow_non_contiguous_dma(reason="one bias value a partition"):
-            nc.sync.dma_start(out=b2_sb[:], in_=b2.rearrange("(c p) -> p c", p=P))
+            nc.sync.dma_start(out=b2_sb, in_=b2.rearrange("(c p) -> p c", p=P))
 
+        early = keep.tile([P, 2, QUARTER, PACK], BF16, name="early", align_bytes=64)
+        late = keep.tile([P, 2, QUARTER, PACK], BF16, name="grouped%d" % (last % 2), align_bytes=64)
         for jq in range(J_QUARTERS):
             square(0, jq)
-        rectify(1, 0, (1, 3))
-        apply_sign(0, 0, "signed0")
+        apply_sign(0, 0, early[:, 0])
         quant_h(0, 0)
-        square(1, 0)
-        apply_sign(0, 1, "grouped1")
-        rectify(1, 1, (1, 3))
+        apply_sign(0, 1, late[:, 0])
+        for t in range(PACK):
+            rectify(1, 0, t, t % 2 == 1)
         quant_h(0, 1)
+        rectify(1, 1, 0, False)
+        square(1, 0)
         square(1, 1)
-        apply_sign(1, 0, "signed0")
+        rectify(1, 1, 1, True)
+        apply_sign(1, 0, early[:, 0])
+        rectify(1, 1, 3, True)
+        rectify(1, 1, 2, False)
         quant_h(1, 0)
-        apply_sign(1, 1, "signed1")
+        apply_sign(1, 1, early[:, 1])
+        apply_sign(0, 2, late[:, 1])
         quant_h(1, 1)
-        stage2(0, ())
-        for jq in range(2, J_QUARTERS):
-            square(1, jq)
-        stage2(1, ())
-        apply_sign(0, 2, "grouped1")
-        apply_sign(0, 3, "signed0")
+        apply_sign(0, 3, late[:, 0])
         quant_h(0, 2)
+        square(1, 2)
+        stage2(0, ())
+        square(1, 3)
+        apply_sign(1, 2, early[:, 0])
         quant_h(0, 3)
-        for jq in range(2, J_QUARTERS):
-            apply_sign(1, jq, "signed%d" % (jq % 2))
-            quant_h(1, jq)
-        for jq in range(2, J_QUARTERS):
-            stage2(jq, (1,))
+        stage2(1, (1,))
+        quant_h(1, 2)
+        apply_sign(1, 3, early[:, 1])
+        stage2(2, (1,))
+        quant_h(1, 3)
+        stage2(3, (1,))

@@ -30,7 +30,11 @@ J_QUARTERS = S // QUARTER
 SIGN_COLS = 64
 BLOCK_WORDS = 8
 STREAM_BUFS = 4
-BLOCK0_CASTS_ON_VECTOR = ((0,), (0,), (64,), (0, 42))
+PIECES = ((256, 256), (256, 256))
+CASTS_ON_VECTOR = (
+    (((0, 0),), ((0, 0),), ((72, 72),), ((36, 36), (42, 42))),
+    (((128, 128),), ((128, 128),), ((128, 128),), ((64, 0), (64, 64))),
+)
 
 
 def tile_list_perturbation_program_scores_kernel(
@@ -80,22 +84,26 @@ def tile_list_perturbation_program_scores_kernel(
             nc.sync.dma_start(out=tabw[a][:].bitcast(I32), in_=tab_words[a].rearrange("p t i -> p (t i)").bitcast(I32))
 
         def load_w1(a, b):
-            pieces = 2 if a == K_PASSES - 1 else 1
-            width = PASS // pieces
-            chunk = stream_tile([P, pieces, PACK, width], F32)
-            for u in range(pieces):
-                raw[a, b, u] = chunk[:, u]
-                c0 = PASS * b + width * u
-                src = w1[PASS * a : PASS * (a + 1), c0 : c0 + width]
+            widths = PIECES[b] if a == K_PASSES - 1 else (PASS,)
+            shared = stream_tile([P, PACK * PASS], F32) if b == 0 else None
+            c0 = 0
+            for u, width in enumerate(widths):
+                if b == 0:
+                    piece = shared[:, PACK * c0 : PACK * (c0 + width)]
+                else:
+                    piece = stream_tile([P, PACK * width], F32)[:]
+                raw[a, b, u] = piece.rearrange("p (j c) -> p j c", j=PACK)
+                src = w1[PASS * a : PASS * (a + 1), PASS * b + c0 : PASS * b + c0 + width]
                 nc.sync.dma_start(out=raw[a, b, u], in_=src.rearrange("(p j) c -> p j c", j=PACK))
+                c0 += width
 
         load_tab(0)
         gain_rows = keep.tile([P, R_PASSES, BLOCK_WORDS], F32, name="gain_rows")
         gain_sb = gain_rows[:, :, 0:PACK]
         nc.sync.dma_start(out=gain_sb, in_=gain.rearrange("(b p t) -> p b t", b=R_PASSES, t=PACK))
 
-        load_w1(0, 0)
         load_tab(1)
+        load_w1(0, 0)
         picked_sc = keep.tile([P, S], U8, name="picked_sc", align_bytes=64)
         nc.vector.tensor_copy(picked_sc[:], tab_sc[:].indirect(offsets[:]))
         for q in range(QUADS):
@@ -129,16 +137,18 @@ def tile_list_perturbation_program_scores_kernel(
         def cast_w1(a, b, on_vector):
             g = keep.tile([P, PACK, P, PACK], BF16, name="grouped%d" % (a % 2), align_bytes=64)
             grouped[a, b] = g
-            groups = P // len(on_vector)
-            for u, split in enumerate(on_vector):
-                for pair in range(PACK // 2):
+            first = 0
+            for u, splits in enumerate(on_vector):
+                groups = raw[a, b, u].shape[2] // PACK
+                for pair, split in enumerate(splits):
                     ts = slice(2 * pair, 2 * pair + 2)
-                    dst = g[:, ts].rearrange("p t m j -> p m j t")[:, groups * u : groups * (u + 1)]
+                    dst = g[:, ts].rearrange("p t m j -> p m j t")[:, first : first + groups]
                     src = raw[a, b, u].rearrange("p j (m t) -> p m j t", t=PACK)[:, :, :, ts]
                     if split > 0:
                         nc.vector.tensor_copy(out=dst[:, 0:split], in_=src[:, 0:split])
                     if split < groups:
                         nc.scalar.activation(out=dst[:, split:groups], in_=src[:, split:groups], func=ACT.Copy)
+                first += groups
 
         def quant_w1(a, b):
             w1_q[a, b] = keep.tile([P, PASS], U32, name="w1q%d%d" % (a, b), align_bytes=64)
@@ -160,7 +170,7 @@ def tile_list_perturbation_program_scores_kernel(
 
         acc = {}
 
-        def stage1(a, b, jh):
+        def stage1(a, b, jh, closes):
             for t in range(PACK):
                 if a == 0:
                     acc[b, jh, t] = psum.tile([P, PASS], F32, name="bank%d" % (PACK * jh + t))
@@ -172,7 +182,7 @@ def tile_list_perturbation_program_scores_kernel(
                     rhs=v_w[a, jh][:].bitcast(E5M2X4),
                     rhs_scale=v_sc[:, a, PASS * jh : PASS * (jh + 1)],
                     start=(a == 0),
-                    stop=(a == K_PASSES - 1),
+                    stop=closes,
                 )
 
         planes = {}
@@ -193,10 +203,11 @@ def tile_list_perturbation_program_scores_kernel(
                 nc.scalar.activation(out=planes[b, jh][:, t, :], in_=acc[b, jh, t][:], func=ACT.Relu, scale=col)
 
         def square(b, jq):
-            woven[b, jq] = keep.tile([P, QUARTER, PACK], BF16, name="woven%d%d" % (b, jq), align_bytes=64)
+            tag = "stream0" if (b, jq) == (0, 3) else "woven%d%d" % (b, jq)
+            woven[b, jq] = keep.tile([P, QUARTER, PACK], BF16, name=tag, align_bytes=64)[:]
             c0 = QUARTER * (jq % 2)
             nc.scalar.activation(
-                out=woven[b, jq][:].rearrange("p (c i) t -> p c t i", i=4),
+                out=woven[b, jq].rearrange("p (c i) t -> p c t i", i=4),
                 in_=planes[b, jq // 2][:, :, c0 : c0 + QUARTER].rearrange("p t (c i) -> p c t i", i=4),
                 func=ACT.Square,
             )
@@ -208,7 +219,7 @@ def tile_list_perturbation_program_scores_kernel(
             reps = QUARTER // SIGN_COLS
             nc.vector.tensor_tensor(
                 out=signed[b, jq].rearrange("p (u c) t -> p u (c t)", u=reps),
-                in0=woven[b, jq][:].rearrange("p (u c) t -> p u (c t)", u=reps),
+                in0=woven[b, jq].rearrange("p (u c) t -> p u (c t)", u=reps),
                 in1=sign[:, b].rearrange("p c t -> p (c t)").unsqueeze(1).to_broadcast([P, reps, SIGN_COLS * PACK]),
                 op=ALU.mult,
             )
@@ -222,15 +233,16 @@ def tile_list_perturbation_program_scores_kernel(
                 in_=signed[b, jq].rearrange("p c t -> p (c t)"),
             )
 
-        def stage2(jq, on_vector):
-            banks = [
-                psum.tile([P, 2, QUARTER], F32, name="bank%d" % (2 * jq + pair)) for pair in range(N_TILES // 2)
-            ]
+        scores = {}
+
+        def stage2(jq):
+            for pair in range(N_TILES // 2):
+                scores[jq, pair] = psum.tile([P, 2, QUARTER], F32, name="bank%d" % (2 * jq + pair))
             for b in range(R_PASSES):
                 for c in range(N_TILES):
                     cols = slice(P * c, P * (c + 1))
                     nc.tensor.matmul_mx(
-                        out=banks[c // 2][:, c % 2, :],
+                        out=scores[jq, c // 2][:, c % 2, :],
                         lhsT=w2_w[:, b, cols].bitcast(E4M3X4),
                         lhsT_scale=w2_sc[4 * b : P, cols],
                         rhs=h_q[b, jq][:].bitcast(E4M3X4),
@@ -238,52 +250,54 @@ def tile_list_perturbation_program_scores_kernel(
                         start=(b == 0 and c % 2 == 0),
                         stop=(b == R_PASSES - 1 and c % 2 == 1),
                     )
-            for pair in range(N_TILES // 2):
-                res = keep.tile([P, 2, QUARTER], F32, name="res%d%d" % (jq, pair))
-                for half in range(2):
-                    c = 2 * pair + half
-                    if pair in on_vector:
-                        nc.vector.tensor_scalar(
-                            out=res[:, half, :], in0=banks[pair][:, half, :], scalar1=b2_rows[:, c, 0:1],
-                            scalar2=None, op0=ALU.add,
-                        )
-                    else:
-                        nc.scalar.activation(
-                            out=res[:, half, :], in_=banks[pair][:, half, :], func=ACT.Identity,
-                            bias=b2_rows[:, c, 0:1],
-                        )
-                rows = out[2 * P * pair : 2 * P * (pair + 1), QUARTER * jq : QUARTER * (jq + 1)]
-                nc.sync.dma_start(out=rows.rearrange("(c p) j -> p c j", p=P), in_=res[:])
+
+        def store(jq, pair, on_vector):
+            res = keep.tile([P, 2, QUARTER], F32, name="res%d%d" % (jq, pair))
+            for half in range(2):
+                c = 2 * pair + half
+                if on_vector:
+                    nc.vector.tensor_scalar(
+                        out=res[:, half, :], in0=scores[jq, pair][:, half, :], scalar1=b2_rows[:, c, 0:1],
+                        scalar2=None, op0=ALU.add,
+                    )
+                else:
+                    nc.scalar.activation(
+                        out=res[:, half, :], in_=scores[jq, pair][:, half, :], func=ACT.Identity,
+                        bias=b2_rows[:, c, 0:1],
+                    )
+            rows = out[2 * P * pair : 2 * P * (pair + 1), QUARTER * jq : QUARTER * (jq + 1)]
+            nc.sync.dma_start(out=rows.rearrange("(c p) j -> p c j", p=P), in_=res[:])
 
         last = K_PASSES - 1
-        load_w1(1, 0)
         load_tab(2)
-        load_w1(2, 0)
+        load_w1(1, 0)
         load_tab(3)
+        load_w1(2, 0)
         load_w1(3, 0)
         for a in range(K_PASSES):
             for jh in range(J_HALVES):
                 gather(a, jh)
             if a == 0:
                 split_gain()
-            cast_w1(a, 0, BLOCK0_CASTS_ON_VECTOR[a])
+            cast_w1(a, 0, CASTS_ON_VECTOR[0][a])
             quant_w1(a, 0)
-            for jh in range(J_HALVES):
-                stage1(a, 0, jh)
+            if a < last - 1:
+                for jh in range(J_HALVES):
+                    stage1(a, 0, jh, False)
+        for jh in range(J_HALVES):
+            stage1(last - 1, 0, jh, False)
+            stage1(last, 0, jh, True)
 
         for jh in range(J_HALVES):
             for t in range(PACK):
                 rectify(0, jh, t, (jh, t) == (0, 1))
         for a in range(K_PASSES):
             load_w1(a, 1)
-            cast_w1(a, 1, (P,) if a < last else (P // 2, P // 2))
+            cast_w1(a, 1, CASTS_ON_VECTOR[1][a])
             quant_w1(a, 1)
-            if a < last - 1:
-                for jh in range(J_HALVES):
-                    stage1(a, 1, jh)
-        for jh in range(J_HALVES):
-            stage1(last - 1, 1, jh)
-            stage1(last, 1, jh)
+        for jh, order in enumerate(((0, 1, 2, 3), (0, 1, 3, 2))):
+            for a in order:
+                stage1(a, 1, jh, a == order[-1])
 
         w2_w = stream_tile([P, R_PASSES, N], U32)
         nc.sync.dma_start(out=w2_w[:].bitcast(I32), in_=w2_words.rearrange("a p c i -> p a (c i)").bitcast(I32))
@@ -296,33 +310,34 @@ def tile_list_perturbation_program_scores_kernel(
         late = keep.tile([P, 2, QUARTER, PACK], BF16, name="grouped%d" % (last % 2), align_bytes=64)
         for jq in range(J_QUARTERS):
             square(0, jq)
-        apply_sign(0, 0, early[:, 0])
-        quant_h(0, 0)
-        apply_sign(0, 1, late[:, 0])
+        apply_sign(0, 0, late[:, 0])
         for t in range(PACK):
             rectify(1, 0, t, t % 2 == 1)
-        quant_h(0, 1)
-        rectify(1, 1, 0, False)
+        quant_h(0, 0)
         square(1, 0)
         square(1, 1)
-        rectify(1, 1, 1, True)
-        apply_sign(1, 0, early[:, 0])
-        rectify(1, 1, 3, True)
-        rectify(1, 1, 2, False)
-        quant_h(1, 0)
-        apply_sign(1, 1, early[:, 1])
-        apply_sign(0, 2, late[:, 1])
-        quant_h(1, 1)
-        apply_sign(0, 3, late[:, 0])
-        quant_h(0, 2)
+        for t in range(PACK):
+            rectify(1, 1, t, t < PACK - 1)
         square(1, 2)
-        stage2(0, ())
         square(1, 3)
+        apply_sign(1, 0, early[:, 0])
+        apply_sign(0, 1, late[:, 1])
+        quant_h(1, 0)
+        stage2(0)
+        apply_sign(1, 1, early[:, 1])
+        quant_h(0, 1)
+        apply_sign(0, 2, late[:, 0])
+        quant_h(1, 1)
+        stage2(1)
         apply_sign(1, 2, early[:, 0])
-        quant_h(0, 3)
-        stage2(1, (1,))
+        quant_h(0, 2)
+        apply_sign(0, 3, late[:, 1])
         quant_h(1, 2)
+        stage2(2)
         apply_sign(1, 3, early[:, 1])
-        stage2(2, (1,))
+        quant_h(0, 3)
         quant_h(1, 3)
-        stage2(3, (1,))
+        stage2(3)
+        for jq in range(J_QUARTERS):
+            for pair in range(N_TILES // 2):
+                store(jq, pair, (jq, pair) == (J_QUARTERS - 1, 1))

@@ -106,7 +106,7 @@ def tile_list_perturbation_program_scores_kernel(
         load_w1(0, 0)
         picked_sc = keep.tile([P, S], U8, name="picked_sc", align_bytes=64)
         nc.vector.tensor_copy(picked_sc[:], tab_sc[:].indirect(offsets[:]))
-        for q in range(QUADS):
+        for q in (0, 2, 1, 3):
             nc.sync.dma_start(
                 out=v_sc[QUAD * q : QUAD * q + 4].bitcast(I32),
                 in_=picked_sc[QUAD + 16 * q : QUAD + 16 * (q + 1), :].bitcast(I32),

@@ -32,7 +32,7 @@ BLOCK_WORDS = 8
 STREAM_BUFS = 4
 PIECES = ((256, 256), (256, 256))
 CASTS_ON_VECTOR = (
-    (((0, 0),), ((0, 0),), ((72, 72),), ((36, 36), (42, 42))),
+    (((64, 64),), ((56, 56),), ((80, 80),), ((42, 42), (42, 42))),
     (((128, 128),), ((128, 128),), ((128, 128),), ((64, 0), (64, 64))),
 )
 
@@ -64,13 +64,6 @@ def tile_list_perturbation_program_scores_kernel(
         nc.gpsimd.memset(tab_sc[3 * QUAD : P, :].bitcast(I32), 0)
         v_sc = keep.tile([P, K_PASSES, S], U8, name="v_sc", align_bytes=64)
         nc.gpsimd.memset(v_sc[:].rearrange("p a j -> p (a j)").bitcast(I32), 0)
-        w2_sc = keep.tile([P, N], U8, name="w2_sc", align_bytes=64)
-        nc.gpsimd.memset(w2_sc[:].bitcast(I32), 0)
-        for q in range(QUADS):
-            nc.gpsimd.dma_start(
-                out=w2_sc[QUAD * q : QUAD * q + 8, :].bitcast(I32),
-                in_=w2_scales[:, 4 * q : 4 * q + 4, :].bitcast(I32),
-            )
 
         raw = {}
         tabw = {}
@@ -115,24 +108,26 @@ def tile_list_perturbation_program_scores_kernel(
         G = R_PASSES * PACK
         g_abs = keep.tile([P, G], F32, name="g_abs")
         root0 = keep.tile([P, G], F32, name="root0")
-        guard = keep.tile([P, G], F32, name="guard")
         recip = keep.tile([P, G], F32, name="recip")
-        quot = keep.tile([P, G], F32, name="quot")
-        twice = keep.tile([P, G], F32, name="twice")
+        half_abs = keep.tile([P, G], F32, name="half_abs")
+        half_root = keep.tile([P, G], F32, name="half_root")
         root = keep.tile([P, G], F32, name="root")
         sign = keep.tile([P, R_PASSES, SIGN_COLS, PACK], BF16, name="sign", align_bytes=64)
 
         def split_gain():
             nc.scalar.activation(out=g_abs[:].rearrange("p (b t) -> p b t", t=PACK), in_=gain_sb, func=ACT.Abs)
-            nc.scalar.activation(out=root0[:], in_=g_abs[:], func=ACT.Sqrt)
+            nc.scalar.activation(out=root0[:], in_=g_abs[:], func=ACT.Sqrt, bias=2e-35)
+            nc.vector.reciprocal(out=recip[:], in_=root0[:])
+            nc.scalar.activation(out=half_abs[:], in_=g_abs[:], func=ACT.Copy, scale=0.5)
+            nc.scalar.activation(out=half_root[:], in_=root0[:], func=ACT.Copy, scale=0.5)
             nc.scalar.activation(
                 out=sign[:], in_=gain_sb.unsqueeze(2).to_broadcast([P, R_PASSES, SIGN_COLS, PACK]), func=ACT.Sign
             )
-            nc.gpsimd.tensor_scalar(out=guard[:], in0=root0[:], scalar1=1e-30, scalar2=None, op0=ALU.max)
-            nc.vector.reciprocal(out=recip[:], in_=guard[:])
-            nc.gpsimd.tensor_tensor(out=quot[:], in0=g_abs[:], in1=recip[:], op=ALU.mult)
-            nc.gpsimd.tensor_tensor(out=twice[:], in0=quot[:], in1=root0[:], op=ALU.add)
-            nc.gpsimd.tensor_scalar(out=root[:], in0=twice[:], scalar1=0.5, scalar2=None, op0=ALU.mult)
+            for c in range(G):
+                col = slice(c, c + 1)
+                nc.scalar.activation(
+                    out=root[:, col], in_=recip[:, col], func=ACT.Identity, scale=half_abs[:, col], bias=half_root[:, col]
+                )
 
         def cast_w1(a, b, on_vector):
             g = keep.tile([P, PACK, P, PACK], BF16, name="grouped%d" % (a % 2), align_bytes=64)
@@ -170,8 +165,8 @@ def tile_list_perturbation_program_scores_kernel(
 
         acc = {}
 
-        def stage1(a, b, jh, closes):
-            for t in range(PACK):
+        def stage1(a, b, jh, closes, planes_t=range(PACK)):
+            for t in planes_t:
                 if a == 0:
                     acc[b, jh, t] = psum.tile([P, PASS], F32, name="bank%d" % (PACK * jh + t))
                 cols = slice(P * t, P * (t + 1))
@@ -270,23 +265,25 @@ def tile_list_perturbation_program_scores_kernel(
 
         last = K_PASSES - 1
         load_tab(2)
-        load_w1(1, 0)
         load_tab(3)
+        load_w1(1, 0)
         load_w1(2, 0)
         load_w1(3, 0)
+        split_gain()
         for a in range(K_PASSES):
-            for jh in range(J_HALVES):
-                gather(a, jh)
-            if a == 0:
-                split_gain()
+            for ahead in ((0, 1), (2, 3), (), ())[a]:
+                for jh in range(J_HALVES):
+                    gather(ahead, jh)
             cast_w1(a, 0, CASTS_ON_VECTOR[0][a])
             quant_w1(a, 0)
             if a < last - 1:
                 for jh in range(J_HALVES):
                     stage1(a, 0, jh, False)
-        for jh in range(J_HALVES):
-            stage1(last - 1, 0, jh, False)
-            stage1(last, 0, jh, True)
+        stage1(last - 1, 0, 0, False)
+        stage1(last, 0, 0, True)
+        for t in range(PACK):
+            stage1(last, 0, 1, False, (t,))
+            stage1(last - 1, 0, 1, True, (t,))
 
         for jh in range(J_HALVES):
             for t in range(PACK):
@@ -299,9 +296,16 @@ def tile_list_perturbation_program_scores_kernel(
             for a in order:
                 stage1(a, 1, jh, a == order[-1])
 
+        w2_sc = stream_tile([P, N], U8)
+        nc.vector.memset(w2_sc[:].bitcast(I32), 0)
+        for q in range(QUADS):
+            nc.sync.dma_start(
+                out=w2_sc[QUAD * q : QUAD * q + 8, :].bitcast(I32),
+                in_=w2_scales[:, 4 * q : 4 * q + 4, :].bitcast(I32),
+            )
         w2_w = stream_tile([P, R_PASSES, N], U32)
         nc.sync.dma_start(out=w2_w[:].bitcast(I32), in_=w2_words.rearrange("a p c i -> p a (c i)").bitcast(I32))
-        b2_rows = stream_tile([P, N_TILES, BLOCK_WORDS], F32)
+        b2_rows = keep.tile([P, N_TILES, BLOCK_WORDS], F32, name="stream1", align_bytes=64)
         b2_sb = b2_rows[:, :, 0]
         with nc.allow_non_contiguous_dma(reason="one bias value a partition"):
             nc.sync.dma_start(out=b2_sb, in_=b2.rearrange("(c p) -> p c", p=P))

@@ -30,10 +30,11 @@ J_QUARTERS = S // QUARTER
 SIGN_COLS = 64
 BLOCK_WORDS = 8
 STREAM_BUFS = 4
-PIECES = ((256, 256), (256, 256))
+EARLY_BANKS = 2
+PIECES = {(3, 0): (256, 128, 128), (0, 1): (256, 256), (3, 1): (256, 256)}
 CASTS_ON_VECTOR = (
-    (((64, 64),), ((56, 56),), ((80, 80),), ((42, 42), (42, 42))),
-    (((128, 128),), ((128, 128),), ((128, 128),), ((64, 0), (64, 64))),
+    (((64, 64),), ((56, 56),), ((80, 80),), ((42, 42), (32, 0), (32, 0))),
+    (((64, 64), (64, 64)), ((128, 128),), ((128, 128),), ((64, 32), (64, 64))),
 )
 
 
@@ -77,11 +78,12 @@ def tile_list_perturbation_program_scores_kernel(
             nc.sync.dma_start(out=tabw[a][:].bitcast(I32), in_=tab_words[a].rearrange("p t i -> p (t i)").bitcast(I32))
 
         def load_w1(a, b):
-            widths = PIECES[b] if a == K_PASSES - 1 else (PASS,)
-            shared = stream_tile([P, PACK * PASS], F32) if b == 0 else None
+            widths = PIECES[a, b] if (a, b) in PIECES else (PASS,)
+            apart = (a, b) == (K_PASSES - 1, 1)
+            shared = None if apart else stream_tile([P, PACK * PASS], F32)
             c0 = 0
             for u, width in enumerate(widths):
-                if b == 0:
+                if not apart:
                     piece = shared[:, PACK * c0 : PACK * (c0 + width)]
                 else:
                     piece = stream_tile([P, PACK * width], F32)[:]
@@ -148,7 +150,7 @@ def tile_list_perturbation_program_scores_kernel(
         def quant_w1(a, b):
             w1_q[a, b] = keep.tile([P, PASS], U32, name="w1q%d%d" % (a, b), align_bytes=64)
             w1_sc[a, b] = keep.tile([P, PASS], U8, name="w1s%d%d" % (a, b), align_bytes=64)
-            pieces = 2
+            pieces = 4 if (a, b) == (K_PASSES - 1, 0) else 2
             width = PASS // pieces
             flat = grouped[a, b][:].rearrange("p t m j -> p (t m j)")
             for u in range(pieces):
@@ -246,16 +248,42 @@ def tile_list_perturbation_program_scores_kernel(
                         stop=(b == R_PASSES - 1 and c % 2 == 1),
                     )
 
-        def store(jq, pair, on_vector):
-            res = keep.tile([P, 2, QUARTER], F32, name="res%d%d" % (jq, pair))
-            for half in range(2):
-                c = 2 * pair + half
-                if on_vector:
+        def last_quarter():
+            jq = J_QUARTERS - 1
+            tiles = [psum.tile([P, QUARTER], F32, name="bank%d" % ((6 + c) % 8)) for c in range(N_TILES)]
+            for b, c in ((0, 0), (0, 1), (1, 0), (1, 1), (0, 2), (1, 2), (0, 3), (1, 3)):
+                cols = slice(P * c, P * (c + 1))
+                nc.tensor.matmul_mx(
+                    out=tiles[c][:],
+                    lhsT=w2_w[:, b, cols].bitcast(E4M3X4),
+                    lhsT_scale=w2_sc[4 * b : P, cols],
+                    rhs=h_q[b, jq][:].bitcast(E4M3X4),
+                    rhs_scale=h_sc[b, jq][:],
+                    start=(b == 0),
+                    stop=(b == R_PASSES - 1),
+                )
+            for c in range(N_TILES):
+                res = keep.tile([P, QUARTER], F32, name="last%d" % c)
+                if c < N_TILES - 1:
                     nc.vector.tensor_scalar(
-                        out=res[:, half, :], in0=scores[jq, pair][:, half, :], scalar1=b2_rows[:, c, 0:1],
-                        scalar2=None, op0=ALU.add,
+                        out=res[:], in0=tiles[c][:], scalar1=b2_rows[:, c, 0:1], scalar2=None, op0=ALU.add
                     )
                 else:
+                    nc.scalar.activation(out=res[:], in_=tiles[c][:], func=ACT.Identity, bias=b2_rows[:, c, 0:1])
+                nc.sync.dma_start(out=out[P * c : P * (c + 1), QUARTER * jq : QUARTER * (jq + 1)], in_=res[:])
+
+        def store(jq, pair, on_vector):
+            res = keep.tile([P, 2, QUARTER], F32, name="res%d%d" % (jq, pair))
+            if on_vector:
+                nc.vector.tensor_tensor(
+                    out=res[:],
+                    in0=scores[jq, pair][:],
+                    in1=b2_rows[:, 2 * pair : 2 * pair + 2, 0:1].to_broadcast([P, 2, QUARTER]),
+                    op=ALU.add,
+                )
+            else:
+                for half in range(2):
+                    c = 2 * pair + half
                     nc.scalar.activation(
                         out=res[:, half, :], in_=scores[jq, pair][:, half, :], func=ACT.Identity,
                         bias=b2_rows[:, c, 0:1],
@@ -292,9 +320,15 @@ def tile_list_perturbation_program_scores_kernel(
             load_w1(a, 1)
             cast_w1(a, 1, CASTS_ON_VECTOR[1][a])
             quant_w1(a, 1)
-        for jh, order in enumerate(((0, 1, 2, 3), (0, 1, 3, 2))):
-            for a in order:
-                stage1(a, 1, jh, a == order[-1])
+        for a in range(K_PASSES):
+            stage1(a, 1, 0, a == last)
+        stage1(0, 1, 1, False)
+        stage1(1, 1, 1, False, range(EARLY_BANKS))
+        for t in range(PACK):
+            stage1(last, 1, 1, False, (t,))
+            if t >= EARLY_BANKS:
+                stage1(1, 1, 1, False, (t,))
+            stage1(last - 1, 1, 1, True, (t,))
 
         w2_sc = stream_tile([P, N], U8)
         nc.vector.memset(w2_sc[:].bitcast(I32), 0)
@@ -323,11 +357,12 @@ def tile_list_perturbation_program_scores_kernel(
         for t in range(PACK):
             rectify(1, 1, t, t < PACK - 1)
         square(1, 2)
-        square(1, 3)
         apply_sign(1, 0, early[:, 0])
         apply_sign(0, 1, late[:, 1])
         quant_h(1, 0)
         stage2(0)
+        store(0, 0, False)
+        square(1, 3)
         apply_sign(1, 1, early[:, 1])
         quant_h(0, 1)
         apply_sign(0, 2, late[:, 0])
@@ -341,7 +376,8 @@ def tile_list_perturbation_program_scores_kernel(
         apply_sign(1, 3, early[:, 1])
         quant_h(0, 3)
         quant_h(1, 3)
-        stage2(3)
-        for jq in range(J_QUARTERS):
+        for jq in range(J_QUARTERS - 1):
             for pair in range(N_TILES // 2):
-                store(jq, pair, (jq, pair) == (J_QUARTERS - 1, 1))
+                if (jq, pair) != (0, 0):
+                    store(jq, pair, False)
+        last_quarter()

@@ -31,10 +31,10 @@ SIGN_COLS = 64
 BLOCK_WORDS = 8
 STREAM_BUFS = 4
 EARLY_BANKS = 2
-PIECES = {(3, 0): (256, 128, 128), (0, 1): (256, 256), (3, 1): (256, 256)}
+PIECES = {(3, 0): (256, 256), (3, 1): (256, 256)}
 CASTS_ON_VECTOR = (
-    (((64, 64),), ((56, 56),), ((80, 80),), ((42, 42), (32, 0), (32, 0))),
-    (((64, 64), (64, 64)), ((128, 128),), ((128, 128),), ((64, 32), (64, 64))),
+    (((64, 64),), ((56, 56),), ((80, 80),), ((42, 42), (42, 42))),
+    (((128, 128),), ((128, 128),), ((128, 128),), ((64, 0), (64, 64))),
 )
 
 
@@ -57,7 +57,7 @@ def tile_list_perturbation_program_scores_kernel(
         nc.sync.dma_start(offsets[:], offs)
 
         tab_sc = stream_tile([P, T], U8)
-        nc.sync.dma_start(
+        nc.scalar.dma_start(
             out=tab_sc[QUAD : 3 * QUAD, :].bitcast(I32),
             in_=tab_scales.rearrange("a q t -> q a t").bitcast(I32),
         )
@@ -95,7 +95,7 @@ def tile_list_perturbation_program_scores_kernel(
         load_tab(0)
         gain_rows = keep.tile([P, R_PASSES, BLOCK_WORDS], F32, name="gain_rows")
         gain_sb = gain_rows[:, :, 0:PACK]
-        nc.sync.dma_start(out=gain_sb, in_=gain.rearrange("(b p t) -> p b t", b=R_PASSES, t=PACK))
+        nc.scalar.dma_start(out=gain_sb, in_=gain.rearrange("(b p t) -> p b t", b=R_PASSES, t=PACK))
 
         load_tab(1)
         load_w1(0, 0)
@@ -150,7 +150,7 @@ def tile_list_perturbation_program_scores_kernel(
         def quant_w1(a, b):
             w1_q[a, b] = keep.tile([P, PASS], U32, name="w1q%d%d" % (a, b), align_bytes=64)
             w1_sc[a, b] = keep.tile([P, PASS], U8, name="w1s%d%d" % (a, b), align_bytes=64)
-            pieces = 4 if (a, b) == (K_PASSES - 1, 0) else 2
+            pieces = 2
             width = PASS // pieces
             flat = grouped[a, b][:].rearrange("p t m j -> p (t m j)")
             for u in range(pieces):

@@ -30,7 +30,6 @@ J_QUARTERS = S // QUARTER
 SIGN_COLS = 64
 BLOCK_WORDS = 8
 STREAM_BUFS = 4
-EARLY_BANKS = 2
 PIECES = {(3, 0): (256, 256), (3, 1): (256, 256)}
 CASTS_ON_VECTOR = (
     (((64, 64),), ((56, 56),), ((80, 80),), ((42, 42), (42, 42))),
@@ -182,6 +181,22 @@ def tile_list_perturbation_program_scores_kernel(
                     stop=closes,
                 )
 
+        def quarter_passes(a, jq, u, opens, closes):
+            if opens:
+                acc[jq, u] = psum.tile([P, 2, QUARTER], F32, name="bank%d" % (2 * jq + u))
+            for e in range(2):
+                cols = slice(P * (2 * u + e), P * (2 * u + e + 1))
+                j0 = QUARTER * (jq % 2)
+                nc.tensor.matmul_mx(
+                    out=acc[jq, u][:, e, :],
+                    lhsT=w1_q[a, 1][:, cols].bitcast(E4M3X4),
+                    lhsT_scale=w1_sc[a, 1][:, cols],
+                    rhs=v_w[a, 1][:, j0 : j0 + QUARTER].bitcast(E5M2X4),
+                    rhs_scale=v_sc[:, a, QUARTER * jq : QUARTER * (jq + 1)],
+                    start=(opens and e == 0),
+                    stop=(closes and e == 1),
+                )
+
         planes = {}
         woven = {}
         h_q = {}
@@ -199,13 +214,32 @@ def tile_list_perturbation_program_scores_kernel(
             else:
                 nc.scalar.activation(out=planes[b, jh][:, t, :], in_=acc[b, jh, t][:], func=ACT.Relu, scale=col)
 
+        def rectify_quarter(jq, u, on_vector):
+            if (1, jq) not in quarters:
+                quarters[1, jq] = keep.tile([P, PACK, QUARTER], F32, name="quarter%d" % jq, align_bytes=64)
+            dst = quarters[1, jq][:, 2 * u : 2 * u + 2, :]
+            roots = root[:, PACK + 2 * u : PACK + 2 * u + 2]
+            if on_vector:
+                nc.vector.scalar_tensor_tensor(
+                    out=dst, in0=acc[jq, u][:], scalar=0.0,
+                    in1=roots.unsqueeze(2).to_broadcast([P, 2, QUARTER]), op0=ALU.max, op1=ALU.mult,
+                )
+            else:
+                for e in range(2):
+                    nc.scalar.activation(
+                        out=dst[:, e, :], in_=acc[jq, u][:, e, :], func=ACT.Relu, scale=roots[:, e : e + 1]
+                    )
+
+        quarters = {}
+
         def square(b, jq):
             tag = "stream0" if (b, jq) == (0, 3) else "woven%d%d" % (b, jq)
             woven[b, jq] = keep.tile([P, QUARTER, PACK], BF16, name=tag, align_bytes=64)[:]
             c0 = QUARTER * (jq % 2)
+            src = quarters[b, jq][:] if (b, jq) in quarters else planes[b, jq // 2][:, :, c0 : c0 + QUARTER]
             nc.scalar.activation(
                 out=woven[b, jq].rearrange("p (c i) t -> p c t i", i=4),
-                in_=planes[b, jq // 2][:, :, c0 : c0 + QUARTER].rearrange("p t (c i) -> p c t i", i=4),
+                in_=src.rearrange("p t (c i) -> p c t i", i=4),
                 func=ACT.Square,
             )
 
@@ -322,13 +356,17 @@ def tile_list_perturbation_program_scores_kernel(
             quant_w1(a, 1)
         for a in range(K_PASSES):
             stage1(a, 1, 0, a == last)
-        stage1(0, 1, 1, False)
-        stage1(1, 1, 1, False, range(EARLY_BANKS))
-        for t in range(PACK):
-            stage1(last, 1, 1, False, (t,))
-            if t >= EARLY_BANKS:
-                stage1(1, 1, 1, False, (t,))
-            stage1(last - 1, 1, 1, True, (t,))
+        for jq in (2, 3):
+            for u in range(2):
+                quarter_passes(0, jq, u, True, False)
+        for u in range(2):
+            quarter_passes(1, 2, u, False, False)
+        for jq in (2, 3):
+            for u in range(2):
+                quarter_passes(last, jq, u, False, False)
+                if jq == 3:
+                    quarter_passes(1, jq, u, False, False)
+                quarter_passes(last - 1, jq, u, False, True)
 
         w2_sc = stream_tile([P, N], U8)
         nc.vector.memset(w2_sc[:].bitcast(I32), 0)
@@ -354,9 +392,11 @@ def tile_list_perturbation_program_scores_kernel(
         quant_h(0, 0)
         square(1, 0)
         square(1, 1)
-        for t in range(PACK):
-            rectify(1, 1, t, t < PACK - 1)
+        rectify_quarter(2, 0, True)
+        rectify_quarter(2, 1, True)
         square(1, 2)
+        rectify_quarter(3, 0, False)
+        rectify_quarter(3, 1, False)
         apply_sign(1, 0, early[:, 0])
         apply_sign(0, 1, late[:, 1])
         quant_h(1, 0)
@@ -370,6 +410,7 @@ def tile_list_perturbation_program_scores_kernel(
         stage2(1)
         apply_sign(1, 2, early[:, 0])
         quant_h(0, 2)
+        store(1, 1, True)
         apply_sign(0, 3, late[:, 1])
         quant_h(1, 2)
         stage2(2)
@@ -378,6 +419,6 @@ def tile_list_perturbation_program_scores_kernel(
         quant_h(1, 3)
         for jq in range(J_QUARTERS - 1):
             for pair in range(N_TILES // 2):
-                if (jq, pair) != (0, 0):
+                if (jq, pair) not in ((0, 0), (1, 1)):
                     store(jq, pair, False)
         last_quarter()

@@ -401,16 +401,16 @@ def tile_list_perturbation_program_scores_kernel(
         apply_sign(0, 1, late[:, 1])
         quant_h(1, 0)
         stage2(0)
-        store(0, 0, False)
+        store(0, 1, False)
         square(1, 3)
         apply_sign(1, 1, early[:, 1])
         quant_h(0, 1)
+        store(0, 0, True)
         apply_sign(0, 2, late[:, 0])
         quant_h(1, 1)
         stage2(1)
         apply_sign(1, 2, early[:, 0])
         quant_h(0, 2)
-        store(1, 1, True)
         apply_sign(0, 3, late[:, 1])
         quant_h(1, 2)
         stage2(2)
@@ -419,6 +419,6 @@ def tile_list_perturbation_program_scores_kernel(
         quant_h(1, 3)
         for jq in range(J_QUARTERS - 1):
             for pair in range(N_TILES // 2):
-                if (jq, pair) not in ((0, 0), (1, 1)):
+                if (jq, pair) not in ((0, 0), (0, 1)):
                     store(jq, pair, False)
         last_quarter()

@@ -49,7 +49,7 @@ def tile_list_perturbation_program_scores_kernel(
 
         def stream_tile(shape, dtype):
             tag = "stream%d" % (len(streamed) % STREAM_BUFS)
-            streamed.append(keep.tile(shape, dtype, name=tag, align_bytes=64))
+            streamed.append(keep.tile(shape, dtype, name=tag, align_bytes=256))
             return streamed[-1]
 
         offsets = keep.tile([P, S // 16], U16, name="offsets")
@@ -62,7 +62,7 @@ def tile_list_perturbation_program_scores_kernel(
         )
         nc.gpsimd.memset(tab_sc[0:QUAD, :].bitcast(I32), 0)
         nc.gpsimd.memset(tab_sc[3 * QUAD : P, :].bitcast(I32), 0)
-        v_sc = keep.tile([P, K_PASSES, S], U8, name="v_sc", align_bytes=64)
+        v_sc = keep.tile([P, K_PASSES, S], U8, name="v_sc", align_bytes=256)
         nc.gpsimd.memset(v_sc[:].rearrange("p a j -> p (a j)").bitcast(I32), 0)
 
         raw = {}
@@ -98,7 +98,7 @@ def tile_list_perturbation_program_scores_kernel(
 
         load_tab(1)
         load_w1(0, 0)
-        picked_sc = keep.tile([P, S], U8, name="picked_sc", align_bytes=64)
+        picked_sc = keep.tile([P, S], U8, name="picked_sc", align_bytes=256)
         nc.vector.tensor_copy(picked_sc[:], tab_sc[:].indirect(offsets[:]))
         for q in (0, 2, 1, 3):
             nc.sync.dma_start(
@@ -113,7 +113,7 @@ def tile_list_perturbation_program_scores_kernel(
         half_abs = keep.tile([P, G], F32, name="half_abs")
         half_root = keep.tile([P, G], F32, name="half_root")
         root = keep.tile([P, G], F32, name="root")
-        sign = keep.tile([P, R_PASSES, SIGN_COLS, PACK], BF16, name="sign", align_bytes=64)
+        sign = keep.tile([P, R_PASSES, SIGN_COLS, PACK], BF16, name="sign", align_bytes=256)
 
         def split_gain():
             nc.scalar.activation(out=g_abs[:].rearrange("p (b t) -> p b t", t=PACK), in_=gain_sb, func=ACT.Abs)
@@ -131,7 +131,7 @@ def tile_list_perturbation_program_scores_kernel(
                 )
 
         def cast_w1(a, b, on_vector):
-            g = keep.tile([P, PACK, P, PACK], BF16, name="grouped%d" % (a % 2), align_bytes=64)
+            g = keep.tile([P, PACK, P, PACK], BF16, name="grouped%d" % (a % 2), align_bytes=256)
             grouped[a, b] = g
             first = 0
             for u, splits in enumerate(on_vector):
@@ -147,8 +147,8 @@ def tile_list_perturbation_program_scores_kernel(
                 first += groups
 
         def quant_w1(a, b):
-            w1_q[a, b] = keep.tile([P, PASS], U32, name="w1q%d%d" % (a, b), align_bytes=64)
-            w1_sc[a, b] = keep.tile([P, PASS], U8, name="w1s%d%d" % (a, b), align_bytes=64)
+            w1_q[a, b] = keep.tile([P, PASS], U32, name="w1q%d%d" % (a, b), align_bytes=256)
+            w1_sc[a, b] = keep.tile([P, PASS], U8, name="w1s%d%d" % (a, b), align_bytes=256)
             pieces = 2
             width = PASS // pieces
             flat = grouped[a, b][:].rearrange("p t m j -> p (t m j)")
@@ -161,7 +161,7 @@ def tile_list_perturbation_program_scores_kernel(
                 )
 
         def gather(a, jh):
-            v_w[a, jh] = keep.tile([P, PASS], U32, name="vw%d%d" % (a, jh), align_bytes=64)
+            v_w[a, jh] = keep.tile([P, PASS], U32, name="vw%d%d" % (a, jh), align_bytes=256)
             nc.vector.tensor_copy(v_w[a, jh][:], tabw[a][:].indirect(offsets[:, 32 * jh : 32 * (jh + 1)]))
 
         acc = {}
@@ -204,7 +204,7 @@ def tile_list_perturbation_program_scores_kernel(
 
         def rectify(b, jh, t, on_vector):
             if (b, jh) not in planes:
-                planes[b, jh] = keep.tile([P, PACK, PASS], F32, name="planes%d%d" % (b, jh), align_bytes=64)
+                planes[b, jh] = keep.tile([P, PACK, PASS], F32, name="planes%d%d" % (b, jh), align_bytes=256)
             col = root[:, PACK * b + t : PACK * b + t + 1]
             if on_vector:
                 nc.vector.tensor_scalar(
@@ -216,7 +216,7 @@ def tile_list_perturbation_program_scores_kernel(
 
         def rectify_quarter(jq, u, on_vector):
             if (1, jq) not in quarters:
-                quarters[1, jq] = keep.tile([P, PACK, QUARTER], F32, name="quarter%d" % jq, align_bytes=64)
+                quarters[1, jq] = keep.tile([P, PACK, QUARTER], F32, name="quarter%d" % jq, align_bytes=256)
             dst = quarters[1, jq][:, 2 * u : 2 * u + 2, :]
             roots = root[:, PACK + 2 * u : PACK + 2 * u + 2]
             if on_vector:
@@ -234,7 +234,7 @@ def tile_list_perturbation_program_scores_kernel(
 
         def square(b, jq):
             tag = "stream0" if (b, jq) == (0, 3) else "woven%d%d" % (b, jq)
-            woven[b, jq] = keep.tile([P, QUARTER, PACK], BF16, name=tag, align_bytes=64)[:]
+            woven[b, jq] = keep.tile([P, QUARTER, PACK], BF16, name=tag, align_bytes=256)[:]
             c0 = QUARTER * (jq % 2)
             src = quarters[b, jq][:] if (b, jq) in quarters else planes[b, jq // 2][:, :, c0 : c0 + QUARTER]
             nc.scalar.activation(
@@ -256,8 +256,8 @@ def tile_list_perturbation_program_scores_kernel(
             )
 
         def quant_h(b, jq):
-            h_q[b, jq] = keep.tile([P, QUARTER], U32, name="hq%d%d" % (b, jq), align_bytes=64)
-            h_sc[b, jq] = keep.tile([P, QUARTER], U8, name="hs%d%d" % (b, jq), align_bytes=64)
+            h_q[b, jq] = keep.tile([P, QUARTER], U32, name="hq%d%d" % (b, jq), align_bytes=256)
+            h_sc[b, jq] = keep.tile([P, QUARTER], U8, name="hs%d%d" % (b, jq), align_bytes=256)
             nc.vector.quantize_mx(
                 out=h_q[b, jq][:].bitcast(E4M3X4),
                 scales=h_sc[b, jq][:],
@@ -377,13 +377,13 @@ def tile_list_perturbation_program_scores_kernel(
             )
         w2_w = stream_tile([P, R_PASSES, N], U32)
         nc.sync.dma_start(out=w2_w[:].bitcast(I32), in_=w2_words.rearrange("a p c i -> p a (c i)").bitcast(I32))
-        b2_rows = keep.tile([P, N_TILES, BLOCK_WORDS], F32, name="stream1", align_bytes=64)
+        b2_rows = keep.tile([P, N_TILES, BLOCK_WORDS], F32, name="stream1", align_bytes=256)
         b2_sb = b2_rows[:, :, 0]
         with nc.allow_non_contiguous_dma(reason="one bias value a partition"):
             nc.sync.dma_start(out=b2_sb, in_=b2.rearrange("(c p) -> p c", p=P))
 
-        early = keep.tile([P, 2, QUARTER, PACK], BF16, name="early", align_bytes=64)
-        late = keep.tile([P, 2, QUARTER, PACK], BF16, name="grouped%d" % (last % 2), align_bytes=64)
+        early = keep.tile([P, 2, QUARTER, PACK], BF16, name="early", align_bytes=256)
+        late = keep.tile([P, 2, QUARTER, PACK], BF16, name="grouped%d" % (last % 2), align_bytes=256)
         for jq in range(J_QUARTERS):
             square(0, jq)
         apply_sign(0, 0, late[:, 0])

@@ -52,7 +52,7 @@ def tile_list_perturbation_program_scores_kernel(
             streamed.append(keep.tile(shape, dtype, name=tag, align_bytes=256))
             return streamed[-1]
 
-        offsets = keep.tile([P, S // 16], U16, name="offsets")
+        offsets = keep.tile([P, S // 16], U16, name="offsets", align_bytes=256)
         nc.sync.dma_start(offsets[:], offs)
 
         tab_sc = stream_tile([P, T], U8)
@@ -92,7 +92,7 @@ def tile_list_perturbation_program_scores_kernel(
                 c0 += width
 
         load_tab(0)
-        gain_rows = keep.tile([P, R_PASSES, BLOCK_WORDS], F32, name="gain_rows")
+        gain_rows = keep.tile([P, R_PASSES, BLOCK_WORDS], F32, name="gain_rows", align_bytes=256)
         gain_sb = gain_rows[:, :, 0:PACK]
         nc.scalar.dma_start(out=gain_sb, in_=gain.rearrange("(b p t) -> p b t", b=R_PASSES, t=PACK))
 
@@ -297,7 +297,7 @@ def tile_list_perturbation_program_scores_kernel(
                     stop=(b == R_PASSES - 1),
                 )
             for c in range(N_TILES):
-                res = keep.tile([P, QUARTER], F32, name="last%d" % c)
+                res = keep.tile([P, QUARTER], F32, name="last%d" % c, align_bytes=256)
                 if c < N_TILES - 1:
                     nc.vector.tensor_scalar(
                         out=res[:], in0=tiles[c][:], scalar1=b2_rows[:, c, 0:1], scalar2=None, op0=ALU.add
@@ -307,7 +307,7 @@ def tile_list_perturbation_program_scores_kernel(
                 nc.sync.dma_start(out=out[P * c : P * (c + 1), QUARTER * jq : QUARTER * (jq + 1)], in_=res[:])
 
         def store(jq, pair, on_vector):
-            res = keep.tile([P, 2, QUARTER], F32, name="res%d%d" % (jq, pair))
+            res = keep.tile([P, 2, QUARTER], F32, name="res%d%d" % (jq, pair), align_bytes=256)
             if on_vector:
                 nc.vector.tensor_tensor(
                     out=res[:],

@@ -32,7 +32,7 @@ BLOCK_WORDS = 8
 STREAM_BUFS = 4
 PIECES = {(3, 0): (256, 256), (3, 1): (256, 256)}
 CASTS_ON_VECTOR = (
-    (((64, 64),), ((56, 56),), ((80, 80),), ((42, 42), (42, 42))),
+    (((0, 0),), ((40, 40),), ((80, 80),), ((42, 42), (42, 42))),
     (((128, 128),), ((128, 128),), ((128, 128),), ((64, 0), (64, 64))),
 )
 
@@ -64,6 +64,9 @@ def tile_list_perturbation_program_scores_kernel(
         nc.gpsimd.memset(tab_sc[3 * QUAD : P, :].bitcast(I32), 0)
         v_sc = keep.tile([P, K_PASSES, S], U8, name="v_sc", align_bytes=256)
         nc.gpsimd.memset(v_sc[:].rearrange("p a j -> p (a j)").bitcast(I32), 0)
+
+        w2_sc = keep.tile([P, N], U8, name="w2_sc", align_bytes=256)
+        nc.gpsimd.memset(w2_sc[:].bitcast(I32), 0)
 
         raw = {}
         tabw = {}
@@ -160,9 +163,11 @@ def tile_list_perturbation_program_scores_kernel(
                     in_=flat[:, PACK * width * u : PACK * width * (u + 1)],
                 )
 
-        def gather(a, jh):
-            v_w[a, jh] = keep.tile([P, PASS], U32, name="vw%d%d" % (a, jh), align_bytes=256)
-            nc.vector.tensor_copy(v_w[a, jh][:], tabw[a][:].indirect(offsets[:, 32 * jh : 32 * (jh + 1)]))
+        def gather(a):
+            picked = keep.tile([P, S], U32, name="vw%d" % a, align_bytes=256)
+            nc.vector.tensor_copy(picked[:], tabw[a][:].indirect(offsets[:]))
+            for jh in range(J_HALVES):
+                v_w[a, jh] = picked[:, PASS * jh : PASS * (jh + 1)]
 
         acc = {}
 
@@ -175,7 +180,7 @@ def tile_list_perturbation_program_scores_kernel(
                     out=acc[b, jh, t][:],
                     lhsT=w1_q[a, b][:, cols].bitcast(E4M3X4),
                     lhsT_scale=w1_sc[a, b][:, cols],
-                    rhs=v_w[a, jh][:].bitcast(E5M2X4),
+                    rhs=v_w[a, jh].bitcast(E5M2X4),
                     rhs_scale=v_sc[:, a, PASS * jh : PASS * (jh + 1)],
                     start=(a == 0),
                     stop=closes,
@@ -334,8 +339,7 @@ def tile_list_perturbation_program_scores_kernel(
         split_gain()
         for a in range(K_PASSES):
             for ahead in ((0, 1), (2, 3), (), ())[a]:
-                for jh in range(J_HALVES):
-                    gather(ahead, jh)
+                gather(ahead)
             cast_w1(a, 0, CASTS_ON_VECTOR[0][a])
             quant_w1(a, 0)
             if a < last - 1:
@@ -368,14 +372,12 @@ def tile_list_perturbation_program_scores_kernel(
                     quarter_passes(1, jq, u, False, False)
                 quarter_passes(last - 1, jq, u, False, True)
 
-        w2_sc = stream_tile([P, N], U8)
-        nc.vector.memset(w2_sc[:].bitcast(I32), 0)
         for q in range(QUADS):
             nc.sync.dma_start(
                 out=w2_sc[QUAD * q : QUAD * q + 8, :].bitcast(I32),
                 in_=w2_scales[:, 4 * q : 4 * q + 4, :].bitcast(I32),
             )
-        w2_w = stream_tile([P, R_PASSES, N], U32)
+        w2_w = keep.tile([P, R_PASSES, N], U32, name="stream3", align_bytes=256)
         nc.sync.dma_start(out=w2_w[:].bitcast(I32), in_=w2_words.rearrange("a p c i -> p a (c i)").bitcast(I32))
         b2_rows = keep.tile([P, N_TILES, BLOCK_WORDS], F32, name="stream1", align_bytes=256)
         b2_sb = b2_rows[:, :, 0]

@@ -30,6 +30,7 @@ J_QUARTERS = S // QUARTER
 SIGN_COLS = 64
 BLOCK_WORDS = 8
 STREAM_BUFS = 4
+SHIFT = 32
 PIECES = {(3, 0): (256, 256), (3, 1): (256, 256)}
 CASTS_ON_VECTOR = (
     (((0, 0),), ((40, 40),), ((80, 80),), ((42, 42), (42, 42))),
@@ -164,8 +165,8 @@ def tile_list_perturbation_program_scores_kernel(
                 )
 
         def gather(a):
-            picked = keep.tile([P, S], U32, name="vw%d" % a, align_bytes=256)
-            nc.vector.tensor_copy(picked[:], tabw[a][:].indirect(offsets[:]))
+            picked = keep.tile([P, SHIFT + S], U32, name="vw%d" % a, align_bytes=256)[:, SHIFT:]
+            nc.vector.tensor_copy(picked, tabw[a][:].indirect(offsets[:]))
             for jh in range(J_HALVES):
                 v_w[a, jh] = picked[:, PASS * jh : PASS * (jh + 1)]
 
@@ -261,10 +262,10 @@ def tile_list_perturbation_program_scores_kernel(
             )
 
         def quant_h(b, jq):
-            h_q[b, jq] = keep.tile([P, QUARTER], U32, name="hq%d%d" % (b, jq), align_bytes=256)
+            h_q[b, jq] = keep.tile([P, SHIFT + QUARTER], U32, name="hq%d%d" % (b, jq), align_bytes=256)[:, SHIFT:]
             h_sc[b, jq] = keep.tile([P, QUARTER], U8, name="hs%d%d" % (b, jq), align_bytes=256)
             nc.vector.quantize_mx(
-                out=h_q[b, jq][:].bitcast(E4M3X4),
+                out=h_q[b, jq].bitcast(E4M3X4),
                 scales=h_sc[b, jq][:],
                 in_=signed[b, jq].rearrange("p c t -> p (c t)"),
             )
@@ -281,7 +282,7 @@ def tile_list_perturbation_program_scores_kernel(
                         out=scores[jq, c // 2][:, c % 2, :],
                         lhsT=w2_w[:, b, cols].bitcast(E4M3X4),
                         lhsT_scale=w2_sc[4 * b : P, cols],
-                        rhs=h_q[b, jq][:].bitcast(E4M3X4),
+                        rhs=h_q[b, jq].bitcast(E4M3X4),
                         rhs_scale=h_sc[b, jq][:],
                         start=(b == 0 and c % 2 == 0),
                         stop=(b == R_PASSES - 1 and c % 2 == 1),
@@ -296,7 +297,7 @@ def tile_list_perturbation_program_scores_kernel(
                     out=tiles[c][:],
                     lhsT=w2_w[:, b, cols].bitcast(E4M3X4),
                     lhsT_scale=w2_sc[4 * b : P, cols],
-                    rhs=h_q[b, jq][:].bitcast(E4M3X4),
+                    rhs=h_q[b, jq].bitcast(E4M3X4),
                     rhs_scale=h_sc[b, jq][:],
                     start=(b == 0),
                     stop=(b == R_PASSES - 1),

@@ -21,17 +21,29 @@ PACK = 4
 PASS = P * PACK
 K_PASSES = K // PASS
 R_PASSES = H // PASS
-J_HALVES = S // PASS
 N_TILES = N // P
 QUAD = 32
 QUADS = P // QUAD
 QUARTER = 256
+EIGHTH = 128
 J_QUARTERS = S // QUARTER
 SIGN_COLS = 64
 BLOCK_WORDS = 8
 STREAM_BUFS = 4
 SHIFT = 32
-PIECES = {(3, 0): (256, 256), (3, 1): (256, 256)}
+LAST = K_PASSES - 1
+
+BANKS = (
+    (
+        ((0,), 0, 512), ((1,), 0, 512), ((2,), 0, 512), ((3,), 0, 512),
+        ((0,), 512, 512), ((1,), 512, 512), ((2,), 512, 512), ((3,), 512, 512),
+    ),
+    (
+        ((0,), 0, 512), ((1,), 0, 512), ((2,), 0, 512), ((3,), 0, 512),
+        ((0, 1, 2, 3), 512, 128), ((0, 1, 2, 3), 640, 128), ((0, 1), 768, 256), ((2, 3), 768, 256),
+    ),
+)
+DIRECT = 2
 CASTS_ON_VECTOR = (
     (((0, 0),), ((40, 40),), ((80, 80),), ((42, 42), (42, 42))),
     (((128, 128),), ((128, 128),), ((128, 128),), ((64, 0), (64, 64))),
@@ -65,7 +77,6 @@ def tile_list_perturbation_program_scores_kernel(
         nc.gpsimd.memset(tab_sc[3 * QUAD : P, :].bitcast(I32), 0)
         v_sc = keep.tile([P, K_PASSES, S], U8, name="v_sc", align_bytes=256)
         nc.gpsimd.memset(v_sc[:].rearrange("p a j -> p (a j)").bitcast(I32), 0)
-
         w2_sc = keep.tile([P, N], U8, name="w2_sc", align_bytes=256)
         nc.gpsimd.memset(w2_sc[:].bitcast(I32), 0)
 
@@ -81,19 +92,16 @@ def tile_list_perturbation_program_scores_kernel(
             nc.sync.dma_start(out=tabw[a][:].bitcast(I32), in_=tab_words[a].rearrange("p t i -> p (t i)").bitcast(I32))
 
         def load_w1(a, b):
-            widths = PIECES[a, b] if (a, b) in PIECES else (PASS,)
-            apart = (a, b) == (K_PASSES - 1, 1)
-            shared = None if apart else stream_tile([P, PACK * PASS], F32)
-            c0 = 0
-            for u, width in enumerate(widths):
-                if not apart:
-                    piece = shared[:, PACK * c0 : PACK * (c0 + width)]
-                else:
-                    piece = stream_tile([P, PACK * width], F32)[:]
+            pieces = len(CASTS_ON_VECTOR[b][a])
+            width = PASS // pieces
+            apart = (a, b) == (LAST, 1)
+            shared = None if apart else stream_tile([P, pieces, PACK * width], F32)
+            for u in range(pieces):
+                piece = stream_tile([P, PACK * width], F32)[:] if apart else shared[:, u]
                 raw[a, b, u] = piece.rearrange("p (j c) -> p j c", j=PACK)
-                src = w1[PASS * a : PASS * (a + 1), PASS * b + c0 : PASS * b + c0 + width]
+                c0 = PASS * b + width * u
+                src = w1[PASS * a : PASS * (a + 1), c0 : c0 + width]
                 nc.sync.dma_start(out=raw[a, b, u], in_=src.rearrange("(p j) c -> p j c", j=PACK))
-                c0 += width
 
         load_tab(0)
         gain_rows = keep.tile([P, R_PASSES, BLOCK_WORDS], F32, name="gain_rows", align_bytes=256)
@@ -134,131 +142,112 @@ def tile_list_perturbation_program_scores_kernel(
                     out=root[:, col], in_=recip[:, col], func=ACT.Identity, scale=half_abs[:, col], bias=half_root[:, col]
                 )
 
-        def cast_w1(a, b, on_vector):
+        def cast_w1(a, b):
             g = keep.tile([P, PACK, P, PACK], BF16, name="grouped%d" % (a % 2), align_bytes=256)
             grouped[a, b] = g
-            first = 0
-            for u, splits in enumerate(on_vector):
-                groups = raw[a, b, u].shape[2] // PACK
+            groups = P // len(CASTS_ON_VECTOR[b][a])
+            for u, splits in enumerate(CASTS_ON_VECTOR[b][a]):
                 for pair, split in enumerate(splits):
                     ts = slice(2 * pair, 2 * pair + 2)
-                    dst = g[:, ts].rearrange("p t m j -> p m j t")[:, first : first + groups]
+                    dst = g[:, ts].rearrange("p t m j -> p m j t")[:, groups * u : groups * (u + 1)]
                     src = raw[a, b, u].rearrange("p j (m t) -> p m j t", t=PACK)[:, :, :, ts]
                     if split > 0:
                         nc.vector.tensor_copy(out=dst[:, 0:split], in_=src[:, 0:split])
                     if split < groups:
                         nc.scalar.activation(out=dst[:, split:groups], in_=src[:, split:groups], func=ACT.Copy)
-                first += groups
 
         def quant_w1(a, b):
             w1_q[a, b] = keep.tile([P, PASS], U32, name="w1q%d%d" % (a, b), align_bytes=256)
             w1_sc[a, b] = keep.tile([P, PASS], U8, name="w1s%d%d" % (a, b), align_bytes=256)
-            pieces = 2
-            width = PASS // pieces
             flat = grouped[a, b][:].rearrange("p t m j -> p (t m j)")
-            for u in range(pieces):
-                cols = slice(width * u, width * (u + 1))
+            for pair in range(2):
+                cols = slice(2 * P * pair, 2 * P * (pair + 1))
                 nc.vector.quantize_mx(
                     out=w1_q[a, b][:, cols].bitcast(E4M3X4),
                     scales=w1_sc[a, b][:, cols],
-                    in_=flat[:, PACK * width * u : PACK * width * (u + 1)],
+                    in_=flat[:, 2 * PASS * pair : 2 * PASS * (pair + 1)],
                 )
 
         def gather(a):
-            picked = keep.tile([P, SHIFT + S], U32, name="vw%d" % a, align_bytes=256)[:, SHIFT:]
-            nc.vector.tensor_copy(picked, tabw[a][:].indirect(offsets[:]))
-            for jh in range(J_HALVES):
-                v_w[a, jh] = picked[:, PASS * jh : PASS * (jh + 1)]
+            v_w[a] = keep.tile([P, SHIFT + S], U32, name="vw%d" % a, align_bytes=256)[:, SHIFT:]
+            nc.vector.tensor_copy(v_w[a], tabw[a][:].indirect(offsets[:]))
 
         acc = {}
 
-        def stage1(a, b, jh, closes, planes_t=range(PACK)):
-            for t in planes_t:
-                if a == 0:
-                    acc[b, jh, t] = psum.tile([P, PASS], F32, name="bank%d" % (PACK * jh + t))
+        def stage1(a, b, bank, closes):
+            ts, j0, width = BANKS[b][bank]
+            if a == 0:
+                acc[b, bank] = psum.tile([P, len(ts), width], F32, name="bank%d" % bank)
+            for e, t in enumerate(ts):
                 cols = slice(P * t, P * (t + 1))
                 nc.tensor.matmul_mx(
-                    out=acc[b, jh, t][:],
+                    out=acc[b, bank][:, e, :],
                     lhsT=w1_q[a, b][:, cols].bitcast(E4M3X4),
                     lhsT_scale=w1_sc[a, b][:, cols],
-                    rhs=v_w[a, jh].bitcast(E5M2X4),
-                    rhs_scale=v_sc[:, a, PASS * jh : PASS * (jh + 1)],
-                    start=(a == 0),
-                    stop=closes,
+                    rhs=v_w[a][:, j0 : j0 + width].bitcast(E5M2X4),
+                    rhs_scale=v_sc[:, a, j0 : j0 + width],
+                    start=(a == 0 and e == 0),
+                    stop=(closes and e == len(ts) - 1),
                 )
 
-        def quarter_passes(a, jq, u, opens, closes):
-            if opens:
-                acc[jq, u] = psum.tile([P, 2, QUARTER], F32, name="bank%d" % (2 * jq + u))
-            for e in range(2):
-                cols = slice(P * (2 * u + e), P * (2 * u + e + 1))
-                j0 = QUARTER * (jq % 2)
-                nc.tensor.matmul_mx(
-                    out=acc[jq, u][:, e, :],
-                    lhsT=w1_q[a, 1][:, cols].bitcast(E4M3X4),
-                    lhsT_scale=w1_sc[a, 1][:, cols],
-                    rhs=v_w[a, 1][:, j0 : j0 + QUARTER].bitcast(E5M2X4),
-                    rhs_scale=v_sc[:, a, QUARTER * jq : QUARTER * (jq + 1)],
-                    start=(opens and e == 0),
-                    stop=(closes and e == 1),
-                )
-
-        planes = {}
+        rooted = {}
         woven = {}
+        signed = {}
         h_q = {}
         h_sc = {}
 
-        def rectify(b, jh, t, on_vector):
-            if (b, jh) not in planes:
-                planes[b, jh] = keep.tile([P, PACK, PASS], F32, name="planes%d%d" % (b, jh), align_bytes=256)
-            col = root[:, PACK * b + t : PACK * b + t + 1]
-            if on_vector:
-                nc.vector.tensor_scalar(
-                    out=planes[b, jh][:, t, :], in0=acc[b, jh, t][:], scalar1=0.0, scalar2=col,
-                    op0=ALU.max, op1=ALU.mult,
-                )
-            else:
-                nc.scalar.activation(out=planes[b, jh][:, t, :], in_=acc[b, jh, t][:], func=ACT.Relu, scale=col)
-
-        def rectify_quarter(jq, u, on_vector):
-            if (1, jq) not in quarters:
-                quarters[1, jq] = keep.tile([P, PACK, QUARTER], F32, name="quarter%d" % jq, align_bytes=256)
-            dst = quarters[1, jq][:, 2 * u : 2 * u + 2, :]
-            roots = root[:, PACK + 2 * u : PACK + 2 * u + 2]
+        def rectify(b, bank, on_vector=False):
+            ts, j0, width = BANKS[b][bank]
+            if (b, j0) not in rooted:
+                rooted[b, j0] = keep.tile([P, PACK, width], F32, name="rooted%d_%d" % (b, j0), align_bytes=256)
+            roots = root[:, PACK * b + ts[0] : PACK * b + ts[-1] + 1]
             if on_vector:
                 nc.vector.scalar_tensor_tensor(
-                    out=dst, in0=acc[jq, u][:], scalar=0.0,
-                    in1=roots.unsqueeze(2).to_broadcast([P, 2, QUARTER]), op0=ALU.max, op1=ALU.mult,
+                    out=rooted[b, j0][:, ts[0] : ts[-1] + 1, :], in0=acc[b, bank][:], scalar=0.0,
+                    in1=roots.unsqueeze(2).to_broadcast([P, len(ts), width]), op0=ALU.max, op1=ALU.mult,
                 )
-            else:
-                for e in range(2):
-                    nc.scalar.activation(
-                        out=dst[:, e, :], in_=acc[jq, u][:, e, :], func=ACT.Relu, scale=roots[:, e : e + 1]
-                    )
-
-        quarters = {}
+                return
+            for e, t in enumerate(ts):
+                nc.scalar.activation(
+                    out=rooted[b, j0][:, t, :], in_=acc[b, bank][:, e, :], func=ACT.Relu, scale=roots[:, e : e + 1]
+                )
 
         def square(b, jq):
-            tag = "stream0" if (b, jq) == (0, 3) else "woven%d%d" % (b, jq)
-            woven[b, jq] = keep.tile([P, QUARTER, PACK], BF16, name=tag, align_bytes=256)[:]
-            c0 = QUARTER * (jq % 2)
-            src = quarters[b, jq][:] if (b, jq) in quarters else planes[b, jq // 2][:, :, c0 : c0 + QUARTER]
+            woven[b, jq] = keep.tile([P, QUARTER, PACK], BF16, name="stream0" if (b, jq) == (0, 3) else "woven%d%d" % (b, jq), align_bytes=256)
+            j0 = QUARTER * jq
+            src = rooted[b, j0][:, :, 0:QUARTER] if (b, j0) in rooted else rooted[b, j0 - QUARTER][:, :, QUARTER:]
             nc.scalar.activation(
-                out=woven[b, jq].rearrange("p (c i) t -> p c t i", i=4),
+                out=woven[b, jq][:].rearrange("p (c i) t -> p c t i", i=4),
                 in_=src.rearrange("p t (c i) -> p c t i", i=4),
                 func=ACT.Square,
             )
-
-        signed = {}
 
         def apply_sign(b, jq, staging):
             signed[b, jq] = staging
             reps = QUARTER // SIGN_COLS
             nc.vector.tensor_tensor(
-                out=signed[b, jq].rearrange("p (u c) t -> p u (c t)", u=reps),
-                in0=woven[b, jq].rearrange("p (u c) t -> p u (c t)", u=reps),
+                out=staging.rearrange("p (u c) t -> p u (c t)", u=reps),
+                in0=woven[b, jq][:].rearrange("p (u c) t -> p u (c t)", u=reps),
                 in1=sign[:, b].rearrange("p c t -> p (c t)").unsqueeze(1).to_broadcast([P, reps, SIGN_COLS * PACK]),
                 op=ALU.mult,
+            )
+
+        gained = {}
+
+        def gain_relu(bank):
+            gained[bank] = keep.tile([P, EIGHTH, PACK], F32, name="gained%d" % bank, align_bytes=256)
+            nc.vector.scalar_tensor_tensor(
+                out=gained[bank][:], in0=acc[1, bank][:].rearrange("p t j -> p j t"), scalar=0.0,
+                in1=gain_sb[:, 1, :].unsqueeze(1).to_broadcast([P, EIGHTH, PACK]), op0=ALU.max, op1=ALU.mult,
+            )
+
+        def times_sum(bank):
+            j0 = BANKS[1][bank][1] - QUARTER * DIRECT
+            if (1, DIRECT) not in signed:
+                signed[1, DIRECT] = keep.tile([P, QUARTER, PACK], BF16, name="direct", align_bytes=256)[:]
+            nc.vector.tensor_tensor(
+                out=signed[1, DIRECT][:, j0 : j0 + EIGHTH, :], in0=acc[1, bank][:].rearrange("p t j -> p j t"),
+                in1=gained[bank][:], op=ALU.mult,
             )
 
         def quant_h(b, jq):
@@ -272,39 +261,35 @@ def tile_list_perturbation_program_scores_kernel(
 
         scores = {}
 
+        def stage2_pass(dst, jq, b, c, start, stop):
+            cols = slice(P * c, P * (c + 1))
+            nc.tensor.matmul_mx(
+                out=dst,
+                lhsT=w2_w[:, b, cols].bitcast(E4M3X4),
+                lhsT_scale=w2_sc[4 * b : P, cols],
+                rhs=h_q[b, jq].bitcast(E4M3X4),
+                rhs_scale=h_sc[b, jq][:],
+                start=start,
+                stop=stop,
+            )
+
         def stage2(jq):
             for pair in range(N_TILES // 2):
                 scores[jq, pair] = psum.tile([P, 2, QUARTER], F32, name="bank%d" % (2 * jq + pair))
             for b in range(R_PASSES):
                 for c in range(N_TILES):
-                    cols = slice(P * c, P * (c + 1))
-                    nc.tensor.matmul_mx(
-                        out=scores[jq, c // 2][:, c % 2, :],
-                        lhsT=w2_w[:, b, cols].bitcast(E4M3X4),
-                        lhsT_scale=w2_sc[4 * b : P, cols],
-                        rhs=h_q[b, jq].bitcast(E4M3X4),
-                        rhs_scale=h_sc[b, jq][:],
-                        start=(b == 0 and c % 2 == 0),
-                        stop=(b == R_PASSES - 1 and c % 2 == 1),
+                    stage2_pass(
+                        scores[jq, c // 2][:, c % 2, :], jq, b, c, b == 0 and c % 2 == 0, b == R_PASSES - 1 and c % 2 == 1
                     )
 
         def last_quarter():
             jq = J_QUARTERS - 1
-            tiles = [psum.tile([P, QUARTER], F32, name="bank%d" % ((6 + c) % 8)) for c in range(N_TILES)]
-            for b, c in ((0, 0), (0, 1), (1, 0), (1, 1), (0, 2), (1, 2), (0, 3), (1, 3)):
-                cols = slice(P * c, P * (c + 1))
-                nc.tensor.matmul_mx(
-                    out=tiles[c][:],
-                    lhsT=w2_w[:, b, cols].bitcast(E4M3X4),
-                    lhsT_scale=w2_sc[4 * b : P, cols],
-                    rhs=h_q[b, jq].bitcast(E4M3X4),
-                    rhs_scale=h_sc[b, jq][:],
-                    start=(b == 0),
-                    stop=(b == R_PASSES - 1),
-                )
+            tiles = [psum.tile([P, QUARTER], F32, name="bank%d" % bank) for bank in (6, 7, 0, 1)]
+            for b, c in ((0, 0), (0, 1), (0, 2), (0, 3), (1, 0), (1, 1), (1, 2), (1, 3)):
+                stage2_pass(tiles[c][:], jq, b, c, b == 0, b == R_PASSES - 1)
             for c in range(N_TILES):
                 res = keep.tile([P, QUARTER], F32, name="last%d" % c, align_bytes=256)
-                if c < N_TILES - 1:
+                if c % 2 == 0:
                     nc.vector.tensor_scalar(
                         out=res[:], in0=tiles[c][:], scalar1=b2_rows[:, c, 0:1], scalar2=None, op0=ALU.add
                     )
@@ -331,47 +316,50 @@ def tile_list_perturbation_program_scores_kernel(
             rows = out[2 * P * pair : 2 * P * (pair + 1), QUARTER * jq : QUARTER * (jq + 1)]
             nc.sync.dma_start(out=rows.rearrange("(c p) j -> p c j", p=P), in_=res[:])
 
-        last = K_PASSES - 1
         load_tab(2)
         load_tab(3)
-        load_w1(1, 0)
-        load_w1(2, 0)
-        load_w1(3, 0)
+        for a in range(1, K_PASSES):
+            load_w1(a, 0)
         split_gain()
         for a in range(K_PASSES):
             for ahead in ((0, 1), (2, 3), (), ())[a]:
                 gather(ahead)
-            cast_w1(a, 0, CASTS_ON_VECTOR[0][a])
+            cast_w1(a, 0)
             quant_w1(a, 0)
-            if a < last - 1:
-                for jh in range(J_HALVES):
-                    stage1(a, 0, jh, False)
-        stage1(last - 1, 0, 0, False)
-        stage1(last, 0, 0, True)
-        for t in range(PACK):
-            stage1(last, 0, 1, False, (t,))
-            stage1(last - 1, 0, 1, True, (t,))
+            if a < LAST - 1:
+                for bank in range(8):
+                    stage1(a, 0, bank, False)
+        for bank in range(4):
+            stage1(LAST - 1, 0, bank, False)
+        for bank in range(4):
+            stage1(LAST, 0, bank, True)
+        for bank in range(4, 8):
+            stage1(LAST, 0, bank, False)
+            stage1(LAST - 1, 0, bank, True)
+        for bank in range(8):
+            rectify(0, bank, bank == 1)
 
-        for jh in range(J_HALVES):
-            for t in range(PACK):
-                rectify(0, jh, t, (jh, t) == (0, 1))
         for a in range(K_PASSES):
             load_w1(a, 1)
-            cast_w1(a, 1, CASTS_ON_VECTOR[1][a])
+            cast_w1(a, 1)
             quant_w1(a, 1)
-        for a in range(K_PASSES):
-            stage1(a, 1, 0, a == last)
-        for jq in (2, 3):
-            for u in range(2):
-                quarter_passes(0, jq, u, True, False)
-        for u in range(2):
-            quarter_passes(1, 2, u, False, False)
-        for jq in (2, 3):
-            for u in range(2):
-                quarter_passes(last, jq, u, False, False)
-                if jq == 3:
-                    quarter_passes(1, jq, u, False, False)
-                quarter_passes(last - 1, jq, u, False, True)
+        for a in range(LAST):
+            for bank in range(4):
+                stage1(a, 1, bank, False)
+        for bank in range(4):
+            stage1(LAST, 1, bank, True)
+        for bank in range(4, 8):
+            stage1(0, 1, bank, False)
+        stage1(1, 1, 4, False)
+
+        def close_late(bank):
+            stage1(LAST, 1, bank, False)
+            if bank >= 5:
+                stage1(1, 1, bank, False)
+            stage1(LAST - 1, 1, bank, True)
+
+        close_late(4)
+        close_late(5)
 
         for q in range(QUADS):
             nc.sync.dma_start(
@@ -386,42 +374,44 @@ def tile_list_perturbation_program_scores_kernel(
             nc.sync.dma_start(out=b2_sb, in_=b2.rearrange("(c p) -> p c", p=P))
 
         early = keep.tile([P, 2, QUARTER, PACK], BF16, name="early", align_bytes=256)
-        late = keep.tile([P, 2, QUARTER, PACK], BF16, name="grouped%d" % (last % 2), align_bytes=256)
+        late = keep.tile([P, 2, QUARTER, PACK], BF16, name="grouped%d" % (LAST % 2), align_bytes=256)
         for jq in range(J_QUARTERS):
             square(0, jq)
         apply_sign(0, 0, late[:, 0])
-        for t in range(PACK):
-            rectify(1, 0, t, t % 2 == 1)
+        for bank in range(4):
+            rectify(1, bank, bank == 1)
+        apply_sign(0, 1, late[:, 1])
         quant_h(0, 0)
         square(1, 0)
         square(1, 1)
-        rectify_quarter(2, 0, True)
-        rectify_quarter(2, 1, True)
-        square(1, 2)
-        rectify_quarter(3, 0, False)
-        rectify_quarter(3, 1, False)
+        gain_relu(4)
+        quant_h(0, 1)
         apply_sign(1, 0, early[:, 0])
-        apply_sign(0, 1, late[:, 1])
+        gain_relu(5)
         quant_h(1, 0)
         stage2(0)
+        close_late(6)
+        close_late(7)
         store(0, 1, False)
+        store(0, 0, False)
+        rectify(1, 6)
+        rectify(1, 7)
         square(1, 3)
         apply_sign(1, 1, early[:, 1])
-        quant_h(0, 1)
-        store(0, 0, True)
-        apply_sign(0, 2, late[:, 0])
+        times_sum(4)
         quant_h(1, 1)
         stage2(1)
-        apply_sign(1, 2, early[:, 0])
-        quant_h(0, 2)
-        apply_sign(0, 3, late[:, 1])
+        times_sum(5)
+        apply_sign(0, 2, late[:, 0])
         quant_h(1, 2)
+        apply_sign(0, 3, late[:, 1])
+        quant_h(0, 2)
         stage2(2)
-        apply_sign(1, 3, early[:, 1])
+        store(1, 0, True)
+        apply_sign(1, 3, early[:, 0])
         quant_h(0, 3)
         quant_h(1, 3)
-        for jq in range(J_QUARTERS - 1):
-            for pair in range(N_TILES // 2):
-                if (jq, pair) not in ((0, 0), (0, 1)):
-                    store(jq, pair, False)
+        store(1, 1, False)
+        store(2, 0, False)
+        store(2, 1, True)
         last_quarter()

@@ -46,7 +46,7 @@ BANKS = (
 DIRECT = 2
 CASTS_ON_VECTOR = (
     (((0, 0),), ((40, 40),), ((80, 80),), ((42, 42), (42, 42))),
-    (((128, 128),), ((128, 128),), ((128, 128),), ((64, 0), (64, 64))),
+    (((64, 64), (64, 64)), ((128, 128),), ((64, 64), (64, 64)), ((64, 64), (64, 64))),
 )
 
 
@@ -213,7 +213,7 @@ def tile_list_perturbation_program_scores_kernel(
                 )
 
         def square(b, jq):
-            woven[b, jq] = keep.tile([P, QUARTER, PACK], BF16, name="stream0" if (b, jq) == (0, 3) else "woven%d%d" % (b, jq), align_bytes=256)
+            woven[b, jq] = keep.tile([P, QUARTER, PACK], BF16, name="woven%d%d" % (b, jq), align_bytes=256)
             j0 = QUARTER * jq
             src = rooted[b, j0][:, :, 0:QUARTER] if (b, j0) in rooted else rooted[b, j0 - QUARTER][:, :, QUARTER:]
             nc.scalar.activation(

@@ -45,7 +45,7 @@ BANKS = (
 )
 DIRECT = 2
 CASTS_ON_VECTOR = (
-    (((0, 0),), ((40, 40),), ((80, 80),), ((42, 42), (42, 42))),
+    (((0, 0),), ((40, 40),), ((128, 128),), ((64, 64), (64, 64))),
     (((64, 64), (64, 64)), ((128, 128),), ((64, 64), (64, 64)), ((64, 64), (64, 64))),
 )
 

from contextlib import ExitStack

import concourse.mybir as mybir

K, T, S, H, N = 2048, 2048, 1024, 1024, 512
FLOPS = 2 * K * H * S + 2 * H * N * S

F32 = mybir.dt.float32
BF16 = mybir.dt.bfloat16
I32 = mybir.dt.int32
U32 = mybir.dt.uint32
U16 = mybir.dt.uint16
U8 = mybir.dt.uint8
E4M3X4 = mybir.dt.float8_e4m3fn_x4
E5M2X4 = mybir.dt.float8_e5m2_x4
ACT = mybir.ActivationFunctionType
ALU = mybir.AluOpType

P = 128
PACK = 4
PASS = P * PACK
K_PASSES = K // PASS
R_PASSES = H // PASS
N_TILES = N // P
QUAD = 32
QUADS = P // QUAD
QUARTER = 256
EIGHTH = 128
J_QUARTERS = S // QUARTER
SIGN_COLS = 64
BLOCK_WORDS = 8
STREAM_BUFS = 4
SHIFT = 32
LAST = K_PASSES - 1

BANKS = (
    (
        ((0,), 0, 512), ((1,), 0, 512), ((2,), 0, 512), ((3,), 0, 512),
        ((0,), 512, 512), ((1,), 512, 512), ((2,), 512, 512), ((3,), 512, 512),
    ),
    (
        ((0,), 0, 512), ((1,), 0, 512), ((2,), 0, 512), ((3,), 0, 512),
        ((0, 1, 2, 3), 512, 128), ((0, 1, 2, 3), 640, 128), ((0, 1), 768, 256), ((2, 3), 768, 256),
    ),
)
DIRECT = 2
CASTS_ON_VECTOR = (
    (((0, 0),), ((40, 40),), ((128, 128),), ((64, 64), (64, 64))),
    (((64, 64), (64, 64)), ((128, 128),), ((64, 64), (64, 64)), ((64, 64), (64, 64))),
)


def tile_list_perturbation_program_scores_kernel(
    tc, tab_words, tab_scales, offs, w1, gain, w2_words, w2_scales, b2, out
):
    nc = tc.nc
    with ExitStack() as ctx:
        keep = ctx.enter_context(tc.tile_pool(name="keep", bufs=1))
        psum = ctx.enter_context(tc.psum_pool(name="psum", bufs=1))

        streamed = []

        def stream_tile(shape, dtype):
            tag = "stream%d" % (len(streamed) % STREAM_BUFS)
            streamed.append(keep.tile(shape, dtype, name=tag, align_bytes=256))
            return streamed[-1]

        offsets = keep.tile([P, S // 16], U16, name="offsets", align_bytes=256)
        nc.sync.dma_start(offsets[:], offs)

        tab_sc = stream_tile([P, T], U8)
        nc.scalar.dma_start(
            out=tab_sc[QUAD : 3 * QUAD, :].bitcast(I32),
            in_=tab_scales.rearrange("a q t -> q a t").bitcast(I32),
        )
        nc.gpsimd.memset(tab_sc[0:QUAD, :].bitcast(I32), 0)
        nc.gpsimd.memset(tab_sc[3 * QUAD : P, :].bitcast(I32), 0)
        v_sc = keep.tile([P, K_PASSES, S], U8, name="v_sc", align_bytes=256)
        nc.gpsimd.memset(v_sc[:].rearrange("p a j -> p (a j)").bitcast(I32), 0)
        w2_sc = keep.tile([P, N], U8, name="w2_sc", align_bytes=256)
        nc.gpsimd.memset(w2_sc[:].bitcast(I32), 0)

        raw = {}
        tabw = {}
        w1_q = {}
        w1_sc = {}
        v_w = {}
        grouped = {}

        def load_tab(a):
            tabw[a] = stream_tile([P, T], U32)
            nc.sync.dma_start(out=tabw[a][:].bitcast(I32), in_=tab_words[a].rearrange("p t i -> p (t i)").bitcast(I32))

        def load_w1(a, b):
            pieces = len(CASTS_ON_VECTOR[b][a])
            width = PASS // pieces
            apart = (a, b) == (LAST, 1)
            shared = None if apart else stream_tile([P, pieces, PACK * width], F32)
            for u in range(pieces):
                piece = stream_tile([P, PACK * width], F32)[:] if apart else shared[:, u]
                raw[a, b, u] = piece.rearrange("p (j c) -> p j c", j=PACK)
                c0 = PASS * b + width * u
                src = w1[PASS * a : PASS * (a + 1), c0 : c0 + width]
                nc.sync.dma_start(out=raw[a, b, u], in_=src.rearrange("(p j) c -> p j c", j=PACK))

        load_tab(0)
        gain_rows = keep.tile([P, R_PASSES, BLOCK_WORDS], F32, name="gain_rows", align_bytes=256)
        gain_sb = gain_rows[:, :, 0:PACK]
        nc.scalar.dma_start(out=gain_sb, in_=gain.rearrange("(b p t) -> p b t", b=R_PASSES, t=PACK))

        load_tab(1)
        load_w1(0, 0)
        picked_sc = keep.tile([P, S], U8, name="picked_sc", align_bytes=256)
        nc.vector.tensor_copy(picked_sc[:], tab_sc[:].indirect(offsets[:]))
        for q in (0, 2, 1, 3):
            nc.sync.dma_start(
                out=v_sc[QUAD * q : QUAD * q + 4].bitcast(I32),
                in_=picked_sc[QUAD + 16 * q : QUAD + 16 * (q + 1), :].bitcast(I32),
            )

        G = R_PASSES * PACK
        g_abs = keep.tile([P, G], F32, name="g_abs")
        root0 = keep.tile([P, G], F32, name="root0")
        recip = keep.tile([P, G], F32, name="recip")
        half_abs = keep.tile([P, G], F32, name="half_abs")
        half_root = keep.tile([P, G], F32, name="half_root")
        root = keep.tile([P, G], F32, name="root")
        sign = keep.tile([P, R_PASSES, SIGN_COLS, PACK], BF16, name="sign", align_bytes=256)

        def split_gain():
            nc.scalar.activation(out=g_abs[:].rearrange("p (b t) -> p b t", t=PACK), in_=gain_sb, func=ACT.Abs)
            nc.scalar.activation(out=root0[:], in_=g_abs[:], func=ACT.Sqrt, bias=2e-35)
            nc.vector.reciprocal(out=recip[:], in_=root0[:])
            nc.scalar.activation(out=half_abs[:], in_=g_abs[:], func=ACT.Copy, scale=0.5)
            nc.scalar.activation(out=half_root[:], in_=root0[:], func=ACT.Copy, scale=0.5)
            nc.scalar.activation(
                out=sign[:], in_=gain_sb.unsqueeze(2).to_broadcast([P, R_PASSES, SIGN_COLS, PACK]), func=ACT.Sign
            )
            for c in range(G):
                col = slice(c, c + 1)
                nc.scalar.activation(
                    out=root[:, col], in_=recip[:, col], func=ACT.Identity, scale=half_abs[:, col], bias=half_root[:, col]
                )

        def cast_w1(a, b):
            g = keep.tile([P, PACK, P, PACK], BF16, name="grouped%d" % (a % 2), align_bytes=256)
            grouped[a, b] = g
            groups = P // len(CASTS_ON_VECTOR[b][a])
            for u, splits in enumerate(CASTS_ON_VECTOR[b][a]):
                for pair, split in enumerate(splits):
                    ts = slice(2 * pair, 2 * pair + 2)
                    dst = g[:, ts].rearrange("p t m j -> p m j t")[:, groups * u : groups * (u + 1)]
                    src = raw[a, b, u].rearrange("p j (m t) -> p m j t", t=PACK)[:, :, :, ts]
                    if split > 0:
                        nc.vector.tensor_copy(out=dst[:, 0:split], in_=src[:, 0:split])
                    if split < groups:
                        nc.scalar.activation(out=dst[:, split:groups], in_=src[:, split:groups], func=ACT.Copy)

        def quant_w1(a, b):
            w1_q[a, b] = keep.tile([P, PASS], U32, name="w1q%d%d" % (a, b), align_bytes=256)
            w1_sc[a, b] = keep.tile([P, PASS], U8, name="w1s%d%d" % (a, b), align_bytes=256)
            flat = grouped[a, b][:].rearrange("p t m j -> p (t m j)")
            for pair in range(2):
                cols = slice(2 * P * pair, 2 * P * (pair + 1))
                nc.vector.quantize_mx(
                    out=w1_q[a, b][:, cols].bitcast(E4M3X4),
                    scales=w1_sc[a, b][:, cols],
                    in_=flat[:, 2 * PASS * pair : 2 * PASS * (pair + 1)],
                )

        def gather(a):
            v_w[a] = keep.tile([P, SHIFT + S], U32, name="vw%d" % a, align_bytes=256)[:, SHIFT:]
            nc.vector.tensor_copy(v_w[a], tabw[a][:].indirect(offsets[:]))

        acc = {}

        def stage1(a, b, bank, closes):
            ts, j0, width = BANKS[b][bank]
            if a == 0:
                acc[b, bank] = psum.tile([P, len(ts), width], F32, name="bank%d" % bank)
            for e, t in enumerate(ts):
                cols = slice(P * t, P * (t + 1))
                nc.tensor.matmul_mx(
                    out=acc[b, bank][:, e, :],
                    lhsT=w1_q[a, b][:, cols].bitcast(E4M3X4),
                    lhsT_scale=w1_sc[a, b][:, cols],
                    rhs=v_w[a][:, j0 : j0 + width].bitcast(E5M2X4),
                    rhs_scale=v_sc[:, a, j0 : j0 + width],
                    start=(a == 0 and e == 0),
                    stop=(closes and e == len(ts) - 1),
                )

        rooted = {}
        woven = {}
        signed = {}
        h_q = {}
        h_sc = {}

        def rectify(b, bank, on_vector=False):
            ts, j0, width = BANKS[b][bank]
            if (b, j0) not in rooted:
                rooted[b, j0] = keep.tile([P, PACK, width], F32, name="rooted%d_%d" % (b, j0), align_bytes=256)
            roots = root[:, PACK * b + ts[0] : PACK * b + ts[-1] + 1]
            if on_vector:
                nc.vector.scalar_tensor_tensor(
                    out=rooted[b, j0][:, ts[0] : ts[-1] + 1, :], in0=acc[b, bank][:], scalar=0.0,
                    in1=roots.unsqueeze(2).to_broadcast([P, len(ts), width]), op0=ALU.max, op1=ALU.mult,
                )
                return
            for e, t in enumerate(ts):
                nc.scalar.activation(
                    out=rooted[b, j0][:, t, :], in_=acc[b, bank][:, e, :], func=ACT.Relu, scale=roots[:, e : e + 1]
                )

        def square(b, jq):
            woven[b, jq] = keep.tile([P, QUARTER, PACK], BF16, name="woven%d%d" % (b, jq), align_bytes=256)
            j0 = QUARTER * jq
            src = rooted[b, j0][:, :, 0:QUARTER] if (b, j0) in rooted else rooted[b, j0 - QUARTER][:, :, QUARTER:]
            nc.scalar.activation(
                out=woven[b, jq][:].rearrange("p (c i) t -> p c t i", i=4),
                in_=src.rearrange("p t (c i) -> p c t i", i=4),
                func=ACT.Square,
            )

        def apply_sign(b, jq, staging):
            signed[b, jq] = staging
            reps = QUARTER // SIGN_COLS
            nc.vector.tensor_tensor(
                out=staging.rearrange("p (u c) t -> p u (c t)", u=reps),
                in0=woven[b, jq][:].rearrange("p (u c) t -> p u (c t)", u=reps),
                in1=sign[:, b].rearrange("p c t -> p (c t)").unsqueeze(1).to_broadcast([P, reps, SIGN_COLS * PACK]),
                op=ALU.mult,
            )

        gained = {}

        def gain_relu(bank):
            gained[bank] = keep.tile([P, EIGHTH, PACK], F32, name="gained%d" % bank, align_bytes=256)
            nc.vector.scalar_tensor_tensor(
                out=gained[bank][:], in0=acc[1, bank][:].rearrange("p t j -> p j t"), scalar=0.0,
                in1=gain_sb[:, 1, :].unsqueeze(1).to_broadcast([P, EIGHTH, PACK]), op0=ALU.max, op1=ALU.mult,
            )

        def times_sum(bank):
            j0 = BANKS[1][bank][1] - QUARTER * DIRECT
            if (1, DIRECT) not in signed:
                signed[1, DIRECT] = keep.tile([P, QUARTER, PACK], BF16, name="direct", align_bytes=256)[:]
            nc.vector.tensor_tensor(
                out=signed[1, DIRECT][:, j0 : j0 + EIGHTH, :], in0=acc[1, bank][:].rearrange("p t j -> p j t"),
                in1=gained[bank][:], op=ALU.mult,
            )

        def quant_h(b, jq):
            h_q[b, jq] = keep.tile([P, SHIFT + QUARTER], U32, name="hq%d%d" % (b, jq), align_bytes=256)[:, SHIFT:]
            h_sc[b, jq] = keep.tile([P, QUARTER], U8, name="hs%d%d" % (b, jq), align_bytes=256)
            nc.vector.quantize_mx(
                out=h_q[b, jq].bitcast(E4M3X4),
                scales=h_sc[b, jq][:],
                in_=signed[b, jq].rearrange("p c t -> p (c t)"),
            )

        scores = {}

        def stage2_pass(dst, jq, b, c, start, stop):
            cols = slice(P * c, P * (c + 1))
            nc.tensor.matmul_mx(
                out=dst,
                lhsT=w2_w[:, b, cols].bitcast(E4M3X4),
                lhsT_scale=w2_sc[4 * b : P, cols],
                rhs=h_q[b, jq].bitcast(E4M3X4),
                rhs_scale=h_sc[b, jq][:],
                start=start,
                stop=stop,
            )

        def stage2(jq):
            for pair in range(N_TILES // 2):
                scores[jq, pair] = psum.tile([P, 2, QUARTER], F32, name="bank%d" % (2 * jq + pair))
            for b in range(R_PASSES):
                for c in range(N_TILES):
                    stage2_pass(
                        scores[jq, c // 2][:, c % 2, :], jq, b, c, b == 0 and c % 2 == 0, b == R_PASSES - 1 and c % 2 == 1
                    )

        def last_quarter():
            jq = J_QUARTERS - 1
            tiles = [psum.tile([P, QUARTER], F32, name="bank%d" % bank) for bank in (6, 7, 0, 1)]
            for b, c in ((0, 0), (0, 1), (0, 2), (0, 3), (1, 0), (1, 1), (1, 2), (1, 3)):
                stage2_pass(tiles[c][:], jq, b, c, b == 0, b == R_PASSES - 1)
            for c in range(N_TILES):
                res = keep.tile([P, QUARTER], F32, name="last%d" % c, align_bytes=256)
                if c % 2 == 0:
                    nc.vector.tensor_scalar(
                        out=res[:], in0=tiles[c][:], scalar1=b2_rows[:, c, 0:1], scalar2=None, op0=ALU.add
                    )
                else:
                    nc.scalar.activation(out=res[:], in_=tiles[c][:], func=ACT.Identity, bias=b2_rows[:, c, 0:1])
                nc.sync.dma_start(out=out[P * c : P * (c + 1), QUARTER * jq : QUARTER * (jq + 1)], in_=res[:])

        def store(jq, pair, on_vector):
            res = keep.tile([P, 2, QUARTER], F32, name="res%d%d" % (jq, pair), align_bytes=256)
            if on_vector:
                nc.vector.tensor_tensor(
                    out=res[:],
                    in0=scores[jq, pair][:],
                    in1=b2_rows[:, 2 * pair : 2 * pair + 2, 0:1].to_broadcast([P, 2, QUARTER]),
                    op=ALU.add,
                )
            else:
                for half in range(2):
                    c = 2 * pair + half
                    nc.scalar.activation(
                        out=res[:, half, :], in_=scores[jq, pair][:, half, :], func=ACT.Identity,
                        bias=b2_rows[:, c, 0:1],
                    )
            rows = out[2 * P * pair : 2 * P * (pair + 1), QUARTER * jq : QUARTER * (jq + 1)]
            nc.sync.dma_start(out=rows.rearrange("(c p) j -> p c j", p=P), in_=res[:])

        load_tab(2)
        load_tab(3)
        for a in range(1, K_PASSES):
            load_w1(a, 0)
        split_gain()
        for a in range(K_PASSES):
            for ahead in ((0, 1), (2, 3), (), ())[a]:
                gather(ahead)
            cast_w1(a, 0)
            quant_w1(a, 0)
            if a < LAST - 1:
                for bank in range(8):
                    stage1(a, 0, bank, False)
        for bank in range(4):
            stage1(LAST - 1, 0, bank, False)
        for bank in range(4):
            stage1(LAST, 0, bank, True)
        for bank in range(4, 8):
            stage1(LAST, 0, bank, False)
            stage1(LAST - 1, 0, bank, True)
        for bank in range(8):
            rectify(0, bank, bank == 1)

        for a in range(K_PASSES):
            load_w1(a, 1)
            cast_w1(a, 1)
            quant_w1(a, 1)
        for a in range(LAST):
            for bank in range(4):
                stage1(a, 1, bank, False)
        for bank in range(4):
            stage1(LAST, 1, bank, True)
        for bank in range(4, 8):
            stage1(0, 1, bank, False)
        stage1(1, 1, 4, False)

        def close_late(bank):
            stage1(LAST, 1, bank, False)
            if bank >= 5:
                stage1(1, 1, bank, False)
            stage1(LAST - 1, 1, bank, True)

        close_late(4)
        close_late(5)

        for q in range(QUADS):
            nc.sync.dma_start(
                out=w2_sc[QUAD * q : QUAD * q + 8, :].bitcast(I32),
                in_=w2_scales[:, 4 * q : 4 * q + 4, :].bitcast(I32),
            )
        w2_w = keep.tile([P, R_PASSES, N], U32, name="stream3", align_bytes=256)
        nc.sync.dma_start(out=w2_w[:].bitcast(I32), in_=w2_words.rearrange("a p c i -> p a (c i)").bitcast(I32))
        b2_rows = keep.tile([P, N_TILES, BLOCK_WORDS], F32, name="stream1", align_bytes=256)
        b2_sb = b2_rows[:, :, 0]
        with nc.allow_non_contiguous_dma(reason="one bias value a partition"):
            nc.sync.dma_start(out=b2_sb, in_=b2.rearrange("(c p) -> p c", p=P))

        early = keep.tile([P, 2, QUARTER, PACK], BF16, name="early", align_bytes=256)
        late = keep.tile([P, 2, QUARTER, PACK], BF16, name="grouped%d" % (LAST % 2), align_bytes=256)
        for jq in range(J_QUARTERS):
            square(0, jq)
        apply_sign(0, 0, late[:, 0])
        for bank in range(4):
            rectify(1, bank, bank == 1)
        apply_sign(0, 1, late[:, 1])
        quant_h(0, 0)
        square(1, 0)
        square(1, 1)
        gain_relu(4)
        quant_h(0, 1)
        apply_sign(1, 0, early[:, 0])
        gain_relu(5)
        quant_h(1, 0)
        stage2(0)
        close_late(6)
        close_late(7)
        store(0, 1, False)
        store(0, 0, False)
        rectify(1, 6)
        rectify(1, 7)
        square(1, 3)
        apply_sign(1, 1, early[:, 1])
        times_sum(4)
        quant_h(1, 1)
        stage2(1)
        times_sum(5)
        apply_sign(0, 2, late[:, 0])
        quant_h(1, 2)
        apply_sign(0, 3, late[:, 1])
        quant_h(0, 2)
        stage2(2)
        store(1, 0, True)
        apply_sign(1, 3, early[:, 0])
        quant_h(0, 3)
        quant_h(1, 3)
        store(1, 1, False)
        store(2, 0, False)
        store(2, 1, True)
        last_quarter()
